import numpy as np
import ml_dtypes


def mxq(x, axis, fmt="e4m3"):
    dtype, down = {"e4m3": (ml_dtypes.float8_e4m3fn, 7), "e5m2": (ml_dtypes.float8_e5m2, 14)}[fmt]
    v = np.moveaxis(np.asarray(x, np.float32).astype(ml_dtypes.bfloat16).astype(np.float64), axis, -1)
    blocks = v.reshape(v.shape[:-1] + (-1, 32))
    amax = np.abs(blocks).max(-1, keepdims=True)
    byte = np.maximum(np.where(amax > 0, np.frexp(amax)[1] - 1 + 127, 0) - down, 1)
    scale = np.exp2(byte - 127.0)
    codes = (blocks / scale).astype(np.float32).astype(dtype).astype(np.float64)
    return np.moveaxis((codes * scale).reshape(v.shape), -1, axis)


WIDE = False


def mx_kscale(k):
    if not WIDE:
        return np.ones(k)
    levels = np.array([10, -10, 5, -5, 0])
    if k % 512:
        return np.exp2(np.random.permutation(np.resize(levels, k // 32))).repeat(32)
    a = np.empty((k // 512, 16))
    for p in range(k // 512):
        a[p, :8] = np.random.permutation(np.resize(levels, 8))
        for g in range(8):
            far = levels[np.abs(levels - a[p, g]) >= 10]
            a[p, g + 8] = far[np.random.randint(len(far))]
    return np.exp2(a.ravel()).repeat(32)


def f64(x):
    return np.asarray(x).astype(np.float64)


def striped(idx):
    return np.tile(idx.reshape(-1, 16).T, (8, 1)).astype(np.uint16)


def unstriped(offs):
    return offs[:16].T.reshape(-1).astype(np.int64)


E2M1 = np.array([0.0, 0.5, 1.0, 1.5, 2.0, 3.0, 4.0, 6.0, -0.0, -0.5, -1.0, -1.5, -2.0, -3.0, -4.0, -6.0])


def pack_weight(w, fmt):
    k, n = w.shape
    w = f64(np.asarray(w, np.float32).astype(ml_dtypes.bfloat16)).reshape(k // 32, 32, n)
    amax = np.abs(w).max(1)
    if fmt == "e4m3":
        byte = np.frexp(amax)[1] - 1 + 127 - 7
    else:
        mant, ex = np.frexp(amax / 6.0)
        byte = np.where(mant > 0.5, ex, ex - 1) + 127
    byte = np.clip(np.where(amax > 0, byte, 1), 1, 254)
    scaled = (w * np.exp2(127.0 - byte)[:, None, :]).reshape(k, n).astype(np.float32)
    by_word = np.ascontiguousarray(scaled.reshape(k // 512, 128, 4, n).transpose(0, 1, 3, 2))
    if fmt == "e4m3":
        words = by_word.astype(ml_dtypes.float8_e4m3fn).view(np.uint8)
    else:
        c = by_word.astype(ml_dtypes.float4_e2m1fn).view(np.uint8) & 0xF
        words = (c[..., 0::2] | (c[..., 1::2] << 4)).reshape(k // 512, 128, 2 * n)
    return np.ascontiguousarray(words), np.ascontiguousarray(byte.astype(np.uint8).reshape(k // 512, 16, n))


def unpack_weight(words, scales, fmt):
    g, _, n = scales.shape
    words = np.ascontiguousarray(words).reshape(g, 128, n, -1)
    if fmt == "e4m3":
        vals = words.view(ml_dtypes.float8_e4m3fn).astype(np.float64)
    else:
        nib = np.empty((g, 128, n, 4), np.uint8)
        nib[..., 0::2] = words & 0xF
        nib[..., 1::2] = words >> 4
        vals = E2M1[nib]
    vals = vals * np.repeat(np.exp2(scales.astype(np.float64) - 127.0), 8, axis=1)[..., None]
    return vals.transpose(0, 1, 3, 2).reshape(g * 512, n)


def gelu(v):
    return 0.5 * v * (1.0 + np.tanh(np.sqrt(2.0 / np.pi) * (v + 0.044715 * v**3)))


def striped8(idx):
    return np.concatenate([v.reshape(-1, 16).T for v in idx]).astype(np.uint16)


def unstriped8(offs):
    return np.stack([offs[16 * g:16 * g + 16].T.reshape(-1) for g in range(8)]).astype(np.int64)


def heads(xT, wgt, idx8):
    k = np.arange(xT.shape[0])
    return wgt[k // 4 % 128] * xT[k[:, None], idx8[k % 512 // 64]]


K, T, S, H, N = 1024, 2048, 1024, 1024, 384

def setup_inputs():
    n = np.random.standard_normal
    s = mx_kscale(K)[:, None]
    u = mx_kscale(H)[:, None]
    xT = (n((K, T)) * s).astype(np.float32)
    wgt = np.repeat(np.random.uniform(0.5, 2.0, (8, S)), 16, axis=0).astype(np.float32)
    offs = striped8(np.stack([np.random.permutation(T)[:S] for _ in range(8)]))
    w1 = (n((K, H)) / np.sqrt(K) / s * u.T).astype(np.float32)
    w2_words, w2_scales = pack_weight(n((K, H)) / np.sqrt(K) / s * u.T, "e2m1")
    w3_words, w3_scales = pack_weight(n((H, N)) / np.sqrt(H) / u, "e4m3")
    b3 = (0.5 * n(N)).astype(np.float32)
    return {"xT": xT, "wgt": wgt, "offs": offs, "w1": w1,
            "w2_words": w2_words, "w2_scales": w2_scales,
            "w3_words": w3_words, "w3_scales": w3_scales, "b3": b3}

def reference(xT, wgt, offs, w1, w2_words, w2_scales, w3_words, w3_scales, b3):
    xg = heads(f64(xT), f64(wgt), unstriped8(offs))
    xq = mxq(xg, 0, "e4m3")
    a = mxq(f64(w1), 0, "e4m3").T @ xq
    b = unpack_weight(w2_words, w2_scales, "e2m1").T @ xq
    h = np.abs(a - np.maximum(b, 0.0))
    y = unpack_weight(w3_words, w3_scales, "e4m3").T @ mxq(h, 0, "e4m3")
    return y + f64(b3)[:, None]

@@ -1,0 +1,295 @@
+from contextlib import ExitStack
+
+import concourse.mybir as mybir
+
+K, T, S, H, N = 1024, 2048, 1024, 1024, 384
+FLOPS = 2 * S * (2 * K * H + H * N)
+
+F32 = mybir.dt.float32
+BF16 = mybir.dt.bfloat16
+I32 = mybir.dt.int32
+U32 = mybir.dt.uint32
+U16 = mybir.dt.uint16
+U8 = mybir.dt.uint8
+FP8X4 = mybir.dt.float8_e4m3fn_x4
+FP4X4 = mybir.dt.float4_e2m1fn_x4
+ALU = mybir.AluOpType
+ACT = mybir.ActivationFunctionType
+
+P = 128
+PACK = 4
+KP = P * PACK
+HALF = 512
+PAIR = 256
+UNIT = 128
+
+
+def tile_list_neighbour_shape_contrast_kernel(
+    tc, xT, wgt, offs, w1, w2_words, w2_scales, w3_words, w3_scales, b3, out
+):
+    nc = tc.nc
+    with ExitStack() as ctx:
+        keep = ctx.enter_context(tc.tile_pool(name="keep", bufs=1))
+        stream = ctx.enter_context(tc.tile_pool(name="stream", bufs=9))
+        gath = ctx.enter_context(tc.tile_pool(name="gath", bufs=4))
+        inter = ctx.enter_context(tc.tile_pool(name="inter", bufs=4))
+        ring = ctx.enter_context(tc.tile_pool(name="ring", bufs=3))
+        psum = ctx.enter_context(tc.psum_pool(name="psum", bufs=8))
+
+        offsets = keep.tile([P, S // 16], U16, name="offsets")
+        nc.sync.dma_start(offsets[:], offs)
+
+        w2_raw = keep.tile([P, 2, 2 * H], U8, name="w2_raw", align_bytes=64)
+        s2_raw = keep.tile([P, 2, H], U8, name="s2_raw", align_bytes=64)
+        w2c = keep.tile([P, 2, 2 * H], U8, name="w2c", align_bytes=64)
+        w2s = keep.tile([P, 2, H], U8, name="w2s", align_bytes=64)
+        w3c = keep.tile([P, 2, N], U32, name="w3c", align_bytes=64)
+        w3s = keep.tile([P, 2, N], U8, name="w3s", align_bytes=64)
+        bias = keep.tile([P, N // P], F32, name="bias")
+        wg = [keep.tile([P, HALF], F32, name="wg%d" % h) for h in range(2)]
+        xc = keep.tile([P, 2, S], U32, name="xc", align_bytes=64)
+        xs = keep.tile([P, 2, S], U8, name="xs", align_bytes=64)
+        w1c = keep.tile([P, 2, H], U32, name="w1c", align_bytes=64)
+        w1s = keep.tile([P, 2, H], U8, name="w1s", align_bytes=64)
+        hc = keep.tile([P, 2, S], U32, name="hc", align_bytes=64)
+        hs = keep.tile([P, 2, S], U8, name="hs", align_bytes=64)
+        rb = {}
+        for cb in range(2):
+            for h in range(2):
+                rb[cb, h] = keep.tile([P, PACK, HALF], F32, name="rb%d%d" % (cb, h))
+
+        nc.vector.memset(s2_raw[:].bitcast(I32), 0)
+        nc.gpsimd.memset(w3s[:].bitcast(I32), 0)
+
+        nc.sync.dma_start(w2_raw[:].bitcast(I32), w2_words.rearrange("a p c -> p a c").bitcast(I32))
+        nc.sync.dma_start(wg[0][:], wgt[:, 0:HALF])
+        for q in range(4):
+            nc.sync.dma_start(
+                s2_raw[32 * q : 32 * q + 4, :, :].bitcast(I32),
+                w2_scales[:, 4 * q : 4 * q + 4, :].rearrange("a q c -> q a c").bitcast(I32),
+            )
+        planes = {}
+        for a in range(2):
+            rows = xT[a * KP : (a + 1) * KP, :].rearrange("(p i) t -> p i t", i=PACK)
+            for i in range(PACK):
+                planes[a, i] = stream.tile([P, T], F32, name="plane", tag="big")
+                nc.sync.dma_start(planes[a, i][:], rows[:, i, :])
+                if (a, i) == (0, 0):
+                    nc.sync.dma_start(wg[1][:], wgt[:, HALF:S])
+        w1_raw = {}
+        for cb in range(2):
+            for a in range(2):
+                w1_raw[cb, a] = stream.tile([P, PACK, KP], F32, name="w1_raw", tag="big")
+                nc.sync.dma_start(
+                    w1_raw[cb, a][:],
+                    w1[a * KP : (a + 1) * KP, cb * KP : (cb + 1) * KP].rearrange("(p j) c -> p j c", j=PACK),
+                )
+        nc.sync.dma_start(
+            w3c[:].bitcast(I32), w3_words.rearrange("a p c i -> p a (c i)").bitcast(I32)
+        )
+        for q in range(4):
+            nc.sync.dma_start(
+                w3s[32 * q : 32 * q + 4, :, :].bitcast(I32),
+                w3_scales[:, 4 * q : 4 * q + 4, :].rearrange("a q c -> q a c").bitcast(I32),
+            )
+        with nc.allow_non_contiguous_dma(reason="one bias value to a partition"):
+            nc.sync.dma_start(bias[:], b3.rearrange("(c p) -> p c", p=P))
+
+        nc.vector.tensor_copy(
+            w2c[:].rearrange("p a c -> p (a c)").bitcast(U16).rearrange("p (g t m) -> p g t m", g=4, t=PACK),
+            w2_raw[:].rearrange("p a c -> p (a c)").bitcast(U16).rearrange("p (g m t) -> p g t m", g=4, t=PACK),
+        )
+        nc.vector.tensor_copy(
+            w2s[:].rearrange("p a (b t m) -> p (a b) t m", b=2, t=PACK),
+            s2_raw[:].rearrange("p a (b m t) -> p (a b) t m", b=2, t=PACK),
+        )
+
+        g4 = {}
+        xb = {}
+
+        def gather(a, i, h, lo, hi):
+            if (a, h) not in g4:
+                g4[a, h] = gath.tile([P, PACK, HALF], F32, name="g4")
+            j0 = h * HALF
+            nc.vector.tensor_tensor(
+                g4[a, h][:, i, lo:hi],
+                planes[a, i][:].indirect(offsets[:, (j0 + lo) // 16 : (j0 + hi) // 16]),
+                wg[h][:, lo:hi],
+                ALU.mult,
+            )
+
+        def weave_x(a, h, lo, hi, on_vector):
+            if (a, h) not in xb:
+                xb[a, h] = inter.tile([P, HALF, PACK], BF16, name="xb", tag="woven", align_bytes=64)
+            dst = xb[a, h][:, lo:hi, :].rearrange("p (c i) t -> p c t i", i=4)
+            src = g4[a, h][:, :, lo:hi].rearrange("p t (c i) -> p c t i", i=4)
+            if on_vector:
+                nc.vector.tensor_copy(dst, src)
+            else:
+                nc.scalar.copy(dst, src)
+
+        def quant_x(a, h):
+            cols = slice(h * HALF, (h + 1) * HALF)
+            nc.vector.quantize_mx(
+                xc[:, a, cols].bitcast(FP8X4), xs[:, a, cols], xb[a, h][:].rearrange("p c t -> p (c t)")
+            )
+
+        wb = {}
+
+        def weave_w1(cb, a, on_vector):
+            wb[cb, a] = inter.tile([P, PACK, P, PACK], BF16, name="wb", tag="woven", align_bytes=64)
+            dst = wb[cb, a][:].rearrange("p t m j -> p m j t")
+            src = w1_raw[cb, a][:].rearrange("p j (m t) -> p m j t", t=PACK)
+            if on_vector:
+                nc.vector.tensor_copy(dst, src)
+            else:
+                nc.scalar.copy(dst, src)
+
+        def quant_w1(cb, a):
+            cols = slice(cb * KP, (cb + 1) * KP)
+            nc.vector.quantize_mx(
+                w1c[:, a, cols].bitcast(FP8X4), w1s[:, a, cols], wb[cb, a][:].rearrange("p t m j -> p (t m j)")
+            )
+
+        bbank = {}
+
+        def b_pass(cb, h, t, a):
+            if a == 0:
+                bbank[cb, h, t] = psum.tile([P, HALF], F32, name="bank", tag="bank")
+            c0 = cb * KP + t * P
+            cols = slice(h * HALF, (h + 1) * HALF)
+            nc.tensor.matmul_mx(
+                bbank[cb, h, t][:],
+                lhsT=w2c[:, a, 2 * c0 : 2 * (c0 + P)].bitcast(FP4X4),
+                lhsT_scale=w2s[:, a, c0 : c0 + P],
+                rhs=xc[:, a, cols].bitcast(FP8X4),
+                rhs_scale=xs[:, a, cols],
+                start=(a == 0),
+                stop=(a == 1),
+            )
+
+        def relu_b(cb, h, t):
+            nc.scalar.activation(rb[cb, h][:, t, :], bbank[cb, h, t][:], ACT.Relu)
+
+        def a_pair(cb, j0):
+            d = ring.tile([P, PACK, PAIR], F32, name="d")
+            cols = slice(j0, j0 + PAIR)
+            jl = j0 % HALF
+            for u in range(2):
+                bank = psum.tile([P, 2, PAIR], F32, name="bank", tag="bank")
+                for v in range(2):
+                    c0 = cb * KP + (2 * u + v) * P
+                    for a in range(2):
+                        nc.tensor.matmul_mx(
+                            bank[:, v, :],
+                            lhsT=w1c[:, a, c0 : c0 + P].bitcast(FP8X4),
+                            lhsT_scale=w1s[:, a, c0 : c0 + P],
+                            rhs=xc[:, a, cols].bitcast(FP8X4),
+                            rhs_scale=xs[:, a, cols],
+                            start=(a == 0),
+                            stop=(a == 1),
+                        )
+                nc.vector.tensor_tensor(
+                    d[:, 2 * u : 2 * u + 2, :],
+                    bank[:],
+                    rb[cb, j0 // HALF][:, 2 * u : 2 * u + 2, jl : jl + PAIR],
+                    ALU.subtract,
+                )
+            hb = ring.tile([P, PAIR, PACK], BF16, name="hb", align_bytes=64)
+            nc.scalar.activation(
+                hb[:].rearrange("p (c i) t -> p c t i", i=4),
+                d[:].rearrange("p t (c i) -> p c t i", i=4),
+                ACT.Abs,
+            )
+            return hb
+
+        def quant_h(cb, j0, hb):
+            cols = slice(j0, j0 + PAIR)
+            nc.vector.quantize_mx(hc[:, cb, cols].bitcast(FP8X4), hs[:, cb, cols], hb[:].rearrange("p c t -> p (c t)"))
+
+        def y_chunk(j0, width, on_vector):
+            cols = slice(j0, j0 + width)
+            res = ring.tile([P, N // P, width], F32, name="res", tag="res", bufs=2)
+            for c in range(N // P):
+                bank = psum.tile([P, width], F32, name="bank", tag="bank")
+                for cb in range(2):
+                    nc.tensor.matmul_mx(
+                        bank[:],
+                        lhsT=w3c[:, cb, c * P : (c + 1) * P].bitcast(FP8X4),
+                        lhsT_scale=w3s[:, cb, c * P : (c + 1) * P],
+                        rhs=hc[:, cb, cols].bitcast(FP8X4),
+                        rhs_scale=hs[:, cb, cols],
+                        start=(cb == 0),
+                        stop=(cb == 1),
+                    )
+                if c in on_vector:
+                    nc.vector.tensor_scalar(res[:, c, :], bank[:], bias[:, c : c + 1], None, ALU.add)
+                else:
+                    nc.scalar.activation(res[:, c, :], bank[:], ACT.Identity, bias=bias[:, c : c + 1])
+                nc.sync.dma_start(out[c * P : (c + 1) * P, cols], res[:, c, :])
+
+        for i in range(PACK):
+            gather(0, i, 0, 0, HALF)
+            gather(0, i, 1, 0, HALF)
+        weave_x(0, 0, 0, HALF, False)
+        weave_x(0, 1, 0, HALF, False)
+        for i in range(PACK - 1):
+            gather(1, i, 0, 0, HALF)
+            if i == 1:
+                quant_x(0, 0)
+        for cb in range(2):
+            for t in range(PACK):
+                b_pass(cb, 0, t, 0)
+        gather(1, 3, 0, 0, PAIR)
+        weave_x(1, 0, 0, PAIR, False)
+        gather(1, 3, 0, PAIR, HALF)
+        weave_x(1, 0, PAIR, HALF, True)
+        quant_x(1, 0)
+        for cb in range(2):
+            for t in range(PACK):
+                b_pass(cb, 0, t, 1)
+        weave_w1(0, 0, True)
+        for t in range(PACK):
+            relu_b(0, 0, t)
+        weave_w1(0, 1, False)
+        gather(1, 0, 1, 0, HALF)
+        quant_w1(0, 0)
+        for i in range(1, PACK):
+            gather(1, i, 1, 0, HALF)
+        quant_x(0, 1)
+        quant_w1(0, 1)
+        weave_x(1, 1, 0, HALF, True)
+        for t in range(PACK):
+            relu_b(1, 0, t)
+        h0 = a_pair(0, 0)
+        quant_x(1, 1)
+        h1 = a_pair(0, 256)
+        for t in range(PACK):
+            b_pass(0, 1, t, 0)
+            b_pass(0, 1, t, 1)
+            relu_b(0, 1, t)
+        weave_w1(1, 0, True)
+        quant_h(0, 0, h0)
+        weave_w1(1, 1, True)
+        quant_w1(1, 0)
+        quant_h(0, 256, h1)
+        quant_w1(1, 1)
+        h2 = a_pair(0, 512)
+        h3 = a_pair(0, 768)
+        for t in range(PACK):
+            b_pass(1, 1, t, 0)
+            b_pass(1, 1, t, 1)
+            relu_b(1, 1, t)
+        quant_h(0, 512, h2)
+        h4 = a_pair(1, 0)
+        quant_h(0, 768, h3)
+        h5 = a_pair(1, 256)
+        quant_h(1, 0, h4)
+        h6 = a_pair(1, 512)
+        quant_h(1, 256, h5)
+        y_chunk(0, HALF, ())
+        h7 = a_pair(1, 768)
+        quant_h(1, 512, h6)
+        y_chunk(512, PAIR, (1,))
+        quant_h(1, 768, h7)
+        y_chunk(768, PAIR, (1,))

@@ -20,8 +20,6 @@ P = 128
 PACK = 4
 KP = P * PACK
 HALF = 512
-PAIR = 256
-UNIT = 128
 
 
 def tile_list_neighbour_shape_contrast_kernel(
@@ -30,17 +28,17 @@ def tile_list_neighbour_shape_contrast_kernel(
     nc = tc.nc
     with ExitStack() as ctx:
         keep = ctx.enter_context(tc.tile_pool(name="keep", bufs=1))
-        stream = ctx.enter_context(tc.tile_pool(name="stream", bufs=9))
+        stream = ctx.enter_context(tc.tile_pool(name="stream", bufs=10))
         gath = ctx.enter_context(tc.tile_pool(name="gath", bufs=4))
-        inter = ctx.enter_context(tc.tile_pool(name="inter", bufs=4))
-        ring = ctx.enter_context(tc.tile_pool(name="ring", bufs=3))
+        inter = ctx.enter_context(tc.tile_pool(name="inter", bufs=7))
+        ring = ctx.enter_context(tc.tile_pool(name="ring", bufs=4))
         psum = ctx.enter_context(tc.psum_pool(name="psum", bufs=8))
 
         offsets = keep.tile([P, S // 16], U16, name="offsets")
         nc.sync.dma_start(offsets[:], offs)
 
-        w2_raw = keep.tile([P, 2, 2 * H], U8, name="w2_raw", align_bytes=64)
-        s2_raw = keep.tile([P, 2, H], U8, name="s2_raw", align_bytes=64)
+        w2_raw = inter.tile([P, 2, 2 * H], U8, name="w2_raw", tag="woven", align_bytes=64)
+        s2_raw = inter.tile([P, 2, H], U8, name="s2_raw", tag="woven", align_bytes=64)
         w2c = keep.tile([P, 2, 2 * H], U8, name="w2c", align_bytes=64)
         w2s = keep.tile([P, 2, H], U8, name="w2s", align_bytes=64)
         w3c = keep.tile([P, 2, N], U32, name="w3c", align_bytes=64)
@@ -61,48 +59,74 @@ def tile_list_neighbour_shape_contrast_kernel(
         nc.vector.memset(s2_raw[:].bitcast(I32), 0)
         nc.gpsimd.memset(w3s[:].bitcast(I32), 0)
 
-        nc.sync.dma_start(w2_raw[:].bitcast(I32), w2_words.rearrange("a p c -> p a c").bitcast(I32))
-        nc.sync.dma_start(wg[0][:], wgt[:, 0:HALF])
+        planes = {}
+        w1_raw = {}
+
+        def load_x(a, i):
+            rows = xT[a * KP : (a + 1) * KP, :].rearrange("(p i) t -> p i t", i=PACK)
+            planes[a, i] = stream.tile([P, T], F32, name="plane", tag="big")
+            nc.sync.dma_start(planes[a, i][:], rows[:, i, :])
+
+        def load_w1(cb, a):
+            w1_raw[cb, a] = stream.tile([P, PACK, KP], F32, name="w1_raw", tag="big")
+            nc.sync.dma_start(
+                w1_raw[cb, a][:],
+                w1[a * KP : (a + 1) * KP, cb * KP : (cb + 1) * KP].rearrange("(p j) c -> p j c", j=PACK),
+            )
+
+        def load_wg(h):
+            nc.sync.dma_start(wg[h][:], wgt[:, h * HALF : (h + 1) * HALF])
+
+        def load_w3():
+            nc.sync.dma_start(w3c[:].bitcast(I32), w3_words.rearrange("a p c i -> p a (c i)").bitcast(I32))
+            for q in range(4):
+                nc.sync.dma_start(
+                    w3s[32 * q : 32 * q + 4, :, :].bitcast(I32),
+                    w3_scales[:, 4 * q : 4 * q + 4, :].rearrange("a q c -> q a c").bitcast(I32),
+                )
+            with nc.allow_non_contiguous_dma(reason="one bias value to a partition"):
+                nc.sync.dma_start(bias[:], b3.rearrange("(c p) -> p c", p=P))
+
+        for a in range(2):
+            nc.sync.dma_start(w2_raw[:, a, :].bitcast(I32), w2_words[a].bitcast(I32))
+        load_wg(0)
         for q in range(4):
             nc.sync.dma_start(
                 s2_raw[32 * q : 32 * q + 4, :, :].bitcast(I32),
                 w2_scales[:, 4 * q : 4 * q + 4, :].rearrange("a q c -> q a c").bitcast(I32),
             )
-        planes = {}
-        for a in range(2):
-            rows = xT[a * KP : (a + 1) * KP, :].rearrange("(p i) t -> p i t", i=PACK)
-            for i in range(PACK):
-                planes[a, i] = stream.tile([P, T], F32, name="plane", tag="big")
-                nc.sync.dma_start(planes[a, i][:], rows[:, i, :])
-                if (a, i) == (0, 0):
-                    nc.sync.dma_start(wg[1][:], wgt[:, HALF:S])
-        w1_raw = {}
-        for cb in range(2):
-            for a in range(2):
-                w1_raw[cb, a] = stream.tile([P, PACK, KP], F32, name="w1_raw", tag="big")
-                nc.sync.dma_start(
-                    w1_raw[cb, a][:],
-                    w1[a * KP : (a + 1) * KP, cb * KP : (cb + 1) * KP].rearrange("(p j) c -> p j c", j=PACK),
-                )
-        nc.sync.dma_start(
-            w3c[:].bitcast(I32), w3_words.rearrange("a p c i -> p a (c i)").bitcast(I32)
-        )
-        for q in range(4):
-            nc.sync.dma_start(
-                w3s[32 * q : 32 * q + 4, :, :].bitcast(I32),
-                w3_scales[:, 4 * q : 4 * q + 4, :].rearrange("a q c -> q a c").bitcast(I32),
-            )
-        with nc.allow_non_contiguous_dma(reason="one bias value to a partition"):
-            nc.sync.dma_start(bias[:], b3.rearrange("(c p) -> p c", p=P))
+        load_x(0, 0)
+        load_wg(1)
+        load_x(0, 1)
+        load_x(0, 2)
+        load_x(0, 3)
+        load_x(1, 0)
+        load_x(1, 1)
+        load_x(1, 2)
+        load_w1(0, 0)
+        load_x(1, 3)
+        load_w1(0, 1)
+        load_w1(1, 0)
+        load_w1(1, 1)
+        load_w3()
 
-        nc.vector.tensor_copy(
-            w2c[:].rearrange("p a c -> p (a c)").bitcast(U16).rearrange("p (g t m) -> p g t m", g=4, t=PACK),
-            w2_raw[:].rearrange("p a c -> p (a c)").bitcast(U16).rearrange("p (g m t) -> p g t m", g=4, t=PACK),
-        )
+        for a in range(2):
+            nc.vector.tensor_copy(
+                w2c[:, a, :].bitcast(U16).rearrange("p (b t m) -> p b t m", b=2, t=PACK),
+                w2_raw[:, a, :].bitcast(U16).rearrange("p (b m t) -> p b t m", b=2, t=PACK),
+            )
         nc.vector.tensor_copy(
             w2s[:].rearrange("p a (b t m) -> p (a b) t m", b=2, t=PACK),
             s2_raw[:].rearrange("p a (b m t) -> p (a b) t m", b=2, t=PACK),
         )
+
+        def cast(dst, src, eng):
+            if eng == "G":
+                nc.gpsimd.tensor_scalar(dst, src, 1.0, 0.0, ALU.mult, ALU.add)
+            elif eng:
+                nc.vector.tensor_copy(dst, src)
+            else:
+                nc.scalar.copy(dst, src)
 
         g4 = {}
         xb = {}
@@ -118,15 +142,12 @@ def tile_list_neighbour_shape_contrast_kernel(
                 ALU.mult,
             )
 
-        def weave_x(a, h, lo, hi, on_vector):
+        def weave_x(a, h, lo, hi, eng):
             if (a, h) not in xb:
                 xb[a, h] = inter.tile([P, HALF, PACK], BF16, name="xb", tag="woven", align_bytes=64)
             dst = xb[a, h][:, lo:hi, :].rearrange("p (c i) t -> p c t i", i=4)
             src = g4[a, h][:, :, lo:hi].rearrange("p t (c i) -> p c t i", i=4)
-            if on_vector:
-                nc.vector.tensor_copy(dst, src)
-            else:
-                nc.scalar.copy(dst, src)
+            cast(dst, src, eng)
 
         def quant_x(a, h):
             cols = slice(h * HALF, (h + 1) * HALF)
@@ -136,14 +157,13 @@ def tile_list_neighbour_shape_contrast_kernel(
 
         wb = {}
 
-        def weave_w1(cb, a, on_vector):
-            wb[cb, a] = inter.tile([P, PACK, P, PACK], BF16, name="wb", tag="woven", align_bytes=64)
-            dst = wb[cb, a][:].rearrange("p t m j -> p m j t")
-            src = w1_raw[cb, a][:].rearrange("p j (m t) -> p m j t", t=PACK)
-            if on_vector:
-                nc.vector.tensor_copy(dst, src)
-            else:
-                nc.scalar.copy(dst, src)
+        def weave_w1(cb, a, eng, lo, hi):
+            if (cb, a) not in wb:
+                wb[cb, a] = inter.tile([P, PACK, P, PACK], BF16, name="wb", tag="woven", align_bytes=64)
+            t0 = lo // 32
+            dst = wb[cb, a][:, t0 : t0 + 2, :, :].rearrange("p t m j -> p m j t")
+            src = w1_raw[cb, a][:].rearrange("p j (m t) -> p m j t", t=PACK)[:, :, :, t0 : t0 + 2]
+            cast(dst, src, eng)
 
         def quant_w1(cb, a):
             cols = slice(cb * KP, (cb + 1) * KP)
@@ -168,49 +188,59 @@ def tile_list_neighbour_shape_contrast_kernel(
                 stop=(a == 1),
             )
 
-        def relu_b(cb, h, t):
-            nc.scalar.activation(rb[cb, h][:, t, :], bbank[cb, h, t][:], ACT.Relu)
+        def relu_b(cb, h, t, eng):
+            if eng:
+                nc.vector.tensor_scalar(rb[cb, h][:, t, :], bbank[cb, h, t][:], 0.0, None, ALU.max)
+            else:
+                nc.scalar.activation(rb[cb, h][:, t, :], bbank[cb, h, t][:], ACT.Relu)
 
-        def a_pair(cb, j0):
-            d = ring.tile([P, PACK, PAIR], F32, name="d")
-            cols = slice(j0, j0 + PAIR)
+        abank = {}
+        hb = {}
+
+        def a_mm(cb, j0, w):
+            per = HALF // w
+            cols = slice(j0, j0 + w)
+            for t in range(PACK):
+                if t % per == 0:
+                    abank[cb, j0, t // per] = psum.tile([P, per, w], F32, name="bank", tag="bank")
+                c0 = cb * KP + t * P
+                for a in range(2):
+                    nc.tensor.matmul_mx(
+                        abank[cb, j0, t // per][:, t % per, :],
+                        lhsT=w1c[:, a, c0 : c0 + P].bitcast(FP8X4),
+                        lhsT_scale=w1s[:, a, c0 : c0 + P],
+                        rhs=xc[:, a, cols].bitcast(FP8X4),
+                        rhs_scale=xs[:, a, cols],
+                        start=(a == 0),
+                        stop=(a == 1),
+                    )
+
+        def sub(cb, j0, w):
+            per = HALF // w
             jl = j0 % HALF
-            for u in range(2):
-                bank = psum.tile([P, 2, PAIR], F32, name="bank", tag="bank")
-                for v in range(2):
-                    c0 = cb * KP + (2 * u + v) * P
-                    for a in range(2):
-                        nc.tensor.matmul_mx(
-                            bank[:, v, :],
-                            lhsT=w1c[:, a, c0 : c0 + P].bitcast(FP8X4),
-                            lhsT_scale=w1s[:, a, c0 : c0 + P],
-                            rhs=xc[:, a, cols].bitcast(FP8X4),
-                            rhs_scale=xs[:, a, cols],
-                            start=(a == 0),
-                            stop=(a == 1),
-                        )
-                nc.vector.tensor_tensor(
-                    d[:, 2 * u : 2 * u + 2, :],
-                    bank[:],
-                    rb[cb, j0 // HALF][:, 2 * u : 2 * u + 2, jl : jl + PAIR],
-                    ALU.subtract,
-                )
-            hb = ring.tile([P, PAIR, PACK], BF16, name="hb", align_bytes=64)
+            for u in range(PACK // per):
+                part = rb[cb, j0 // HALF][:, u * per : (u + 1) * per, jl : jl + w]
+                nc.vector.tensor_tensor(part, abank[cb, j0, u][:], part, ALU.subtract)
+
+        def absw(cb, j0, lo, hi):
+            jl = j0 % HALF
+            hb[cb, j0] = ring.tile([P, hi, PACK], BF16, name="hb", tag="hb", align_bytes=64)
             nc.scalar.activation(
-                hb[:].rearrange("p (c i) t -> p c t i", i=4),
-                d[:].rearrange("p t (c i) -> p c t i", i=4),
+                hb[cb, j0][:].rearrange("p (c i) t -> p c t i", i=4),
+                rb[cb, j0 // HALF][:, :, jl : jl + hi].rearrange("p t (c i) -> p c t i", i=4),
                 ACT.Abs,
             )
-            return hb
 
-        def quant_h(cb, j0, hb):
-            cols = slice(j0, j0 + PAIR)
-            nc.vector.quantize_mx(hc[:, cb, cols].bitcast(FP8X4), hs[:, cb, cols], hb[:].rearrange("p c t -> p (c t)"))
+        def quant_h(cb, j0, w):
+            cols = slice(j0, j0 + w)
+            nc.vector.quantize_mx(
+                hc[:, cb, cols].bitcast(FP8X4), hs[:, cb, cols], hb[cb, j0][:].rearrange("p c t -> p (c t)")
+            )
 
         def y_chunk(j0, width, on_vector):
             cols = slice(j0, j0 + width)
-            res = ring.tile([P, N // P, width], F32, name="res", tag="res", bufs=2)
             for c in range(N // P):
+                res = ring.tile([P, width], F32, name="res", tag="res")
                 bank = psum.tile([P, width], F32, name="bank", tag="bank")
                 for cb in range(2):
                     nc.tensor.matmul_mx(
@@ -223,73 +253,134 @@ def tile_list_neighbour_shape_contrast_kernel(
                         stop=(cb == 1),
                     )
                 if c in on_vector:
-                    nc.vector.tensor_scalar(res[:, c, :], bank[:], bias[:, c : c + 1], None, ALU.add)
+                    nc.vector.tensor_scalar(res[:], bank[:], bias[:, c : c + 1], None, ALU.add)
                 else:
-                    nc.scalar.activation(res[:, c, :], bank[:], ACT.Identity, bias=bias[:, c : c + 1])
-                nc.sync.dma_start(out[c * P : (c + 1) * P, cols], res[:, c, :])
+                    nc.scalar.activation(res[:], bank[:], ACT.Identity, bias=bias[:, c : c + 1])
+                nc.sync.dma_start(out[c * P : (c + 1) * P, cols], res[:])
 
-        for i in range(PACK):
-            gather(0, i, 0, 0, HALF)
-            gather(0, i, 1, 0, HALF)
-        weave_x(0, 0, 0, HALF, False)
-        weave_x(0, 1, 0, HALF, False)
-        for i in range(PACK - 1):
-            gather(1, i, 0, 0, HALF)
-            if i == 1:
-                quant_x(0, 0)
-        for cb in range(2):
-            for t in range(PACK):
-                b_pass(cb, 0, t, 0)
-        gather(1, 3, 0, 0, PAIR)
-        weave_x(1, 0, 0, PAIR, False)
-        gather(1, 3, 0, PAIR, HALF)
-        weave_x(1, 0, PAIR, HALF, True)
-        quant_x(1, 0)
-        for cb in range(2):
-            for t in range(PACK):
-                b_pass(cb, 0, t, 1)
-        weave_w1(0, 0, True)
-        for t in range(PACK):
-            relu_b(0, 0, t)
-        weave_w1(0, 1, False)
-        gather(1, 0, 1, 0, HALF)
-        quant_w1(0, 0)
-        for i in range(1, PACK):
-            gather(1, i, 1, 0, HALF)
+        gather(0, 0, 0, 0, 512)
+        gather(0, 0, 1, 0, 512)
+        gather(0, 1, 0, 0, 512)
+        gather(0, 1, 1, 0, 512)
+        gather(0, 2, 0, 0, 512)
+        gather(0, 2, 1, 0, 512)
+        gather(0, 3, 0, 0, 512)
+        gather(0, 3, 1, 0, 512)
+        weave_x(0, 0, 0, 512, False)
+        weave_x(0, 1, 0, 512, False)
+        gather(1, 0, 0, 0, 512)
+        gather(1, 0, 1, 0, 512)
+        gather(1, 1, 0, 0, 512)
+        gather(1, 1, 1, 0, 512)
+        gather(1, 2, 0, 0, 512)
+        gather(1, 2, 1, 0, 512)
+        weave_w1(0, 0, False, 0, 64)
+        weave_w1(0, 0, False, 64, 128)
+        quant_x(0, 0)
+        b_pass(0, 0, 0, 0)
+        b_pass(0, 0, 1, 0)
+        b_pass(0, 0, 2, 0)
+        b_pass(0, 0, 3, 0)
+        b_pass(1, 0, 0, 0)
+        b_pass(1, 0, 1, 0)
+        b_pass(1, 0, 2, 0)
+        b_pass(1, 0, 3, 0)
+        gather(1, 3, 0, 0, 256)
+        weave_x(1, 0, 0, 256, False)
+        gather(1, 3, 0, 256, 512)
+        weave_x(1, 0, 256, 512, True)
+        gather(1, 3, 1, 0, 512)
         quant_x(0, 1)
-        quant_w1(0, 1)
-        weave_x(1, 1, 0, HALF, True)
-        for t in range(PACK):
-            relu_b(1, 0, t)
-        h0 = a_pair(0, 0)
+        quant_x(1, 0)
+        b_pass(0, 0, 0, 1)
+        b_pass(0, 0, 1, 1)
+        b_pass(0, 0, 2, 1)
+        b_pass(0, 0, 3, 1)
+        b_pass(1, 0, 0, 1)
+        b_pass(1, 0, 1, 1)
+        b_pass(1, 0, 2, 1)
+        b_pass(1, 0, 3, 1)
+        weave_x(1, 1, 0, 256, True)
+        weave_x(1, 1, 256, 512, True)
+        quant_w1(0, 0)
         quant_x(1, 1)
-        h1 = a_pair(0, 256)
-        for t in range(PACK):
-            b_pass(0, 1, t, 0)
-            b_pass(0, 1, t, 1)
-            relu_b(0, 1, t)
-        weave_w1(1, 0, True)
-        quant_h(0, 0, h0)
-        weave_w1(1, 1, True)
+        relu_b(0, 0, 0, True)
+        relu_b(0, 0, 1, False)
+        relu_b(0, 0, 2, False)
+        relu_b(0, 0, 3, False)
+        weave_w1(0, 1, False, 0, 64)
+        weave_w1(0, 1, True, 64, 128)
+        quant_w1(0, 1)
+        b_pass(0, 1, 0, 0)
+        b_pass(0, 1, 0, 1)
+        b_pass(0, 1, 1, 0)
+        b_pass(0, 1, 1, 1)
+        b_pass(0, 1, 2, 0)
+        b_pass(0, 1, 2, 1)
+        b_pass(0, 1, 3, 0)
+        b_pass(0, 1, 3, 1)
+        relu_b(1, 0, 0, False)
+        relu_b(1, 0, 1, False)
+        relu_b(1, 0, 2, False)
+        relu_b(1, 0, 3, False)
+        a_mm(0, 0, 256)
+        sub(0, 0, 256)
+        absw(0, 0, 0, 256)
+        a_mm(0, 256, 256)
+        sub(0, 256, 256)
+        absw(0, 256, 0, 256)
+        relu_b(0, 1, 0, False)
+        relu_b(0, 1, 1, True)
+        relu_b(0, 1, 2, False)
+        relu_b(0, 1, 3, True)
+        weave_w1(1, 0, True, 0, 64)
+        weave_w1(1, 0, False, 64, 128)
+        weave_w1(1, 1, True, 0, 64)
+        weave_w1(1, 1, False, 64, 128)
+        b_pass(1, 1, 0, 0)
+        b_pass(1, 1, 0, 1)
+        b_pass(1, 1, 1, 0)
+        b_pass(1, 1, 1, 1)
+        b_pass(1, 1, 2, 0)
+        b_pass(1, 1, 2, 1)
+        b_pass(1, 1, 3, 0)
+        b_pass(1, 1, 3, 1)
+        quant_h(0, 0, 256)
         quant_w1(1, 0)
-        quant_h(0, 256, h1)
         quant_w1(1, 1)
-        h2 = a_pair(0, 512)
-        h3 = a_pair(0, 768)
-        for t in range(PACK):
-            b_pass(1, 1, t, 0)
-            b_pass(1, 1, t, 1)
-            relu_b(1, 1, t)
-        quant_h(0, 512, h2)
-        h4 = a_pair(1, 0)
-        quant_h(0, 768, h3)
-        h5 = a_pair(1, 256)
-        quant_h(1, 0, h4)
-        h6 = a_pair(1, 512)
-        quant_h(1, 256, h5)
-        y_chunk(0, HALF, ())
-        h7 = a_pair(1, 768)
-        quant_h(1, 512, h6)
-        y_chunk(512, PAIR, (1,))
-        quant_h(1, 768, h7)
-        y_chunk(768, PAIR, (1,))
+        quant_h(0, 256, 256)
+        a_mm(0, 512, 256)
+        sub(0, 512, 256)
+        absw(0, 512, 0, 256)
+        a_mm(0, 768, 256)
+        sub(0, 768, 256)
+        absw(0, 768, 0, 256)
+        relu_b(1, 1, 0, False)
+        relu_b(1, 1, 1, False)
+        relu_b(1, 1, 2, False)
+        relu_b(1, 1, 3, False)
+        a_mm(1, 0, 256)
+        sub(1, 0, 256)
+        absw(1, 0, 0, 256)
+        quant_h(0, 512, 256)
+        a_mm(1, 256, 256)
+        sub(1, 256, 256)
+        absw(1, 256, 0, 256)
+        quant_h(0, 768, 256)
+        quant_h(1, 0, 256)
+        a_mm(1, 512, 256)
+        sub(1, 512, 256)
+        absw(1, 512, 0, 256)
+        quant_h(1, 256, 256)
+        y_chunk(0, 512, (0, 2))
+        a_mm(1, 768, 128)
+        sub(1, 768, 128)
+        absw(1, 768, 0, 128)
+        quant_h(1, 512, 256)
+        a_mm(1, 896, 128)
+        sub(1, 896, 128)
+        absw(1, 896, 0, 128)
+        y_chunk(512, 256, (0, 2))
+        quant_h(1, 768, 128)
+        quant_h(1, 896, 128)
+        y_chunk(768, 256, (0, 2))

@@ -37,8 +37,6 @@ def tile_list_neighbour_shape_contrast_kernel(
         offsets = keep.tile([P, S // 16], U16, name="offsets")
         nc.sync.dma_start(offsets[:], offs)
 
-        w2_raw = inter.tile([P, 2, 2 * H], U8, name="w2_raw", tag="woven", align_bytes=64)
-        s2_raw = inter.tile([P, 2, H], U8, name="s2_raw", tag="woven", align_bytes=64)
         w2c = keep.tile([P, 2, 2 * H], U8, name="w2c", align_bytes=64)
         w2s = keep.tile([P, 2, H], U8, name="w2s", align_bytes=64)
         w3c = keep.tile([P, 2, N], U32, name="w3c", align_bytes=64)
@@ -56,7 +54,6 @@ def tile_list_neighbour_shape_contrast_kernel(
             for h in range(2):
                 rb[cb, h] = keep.tile([P, PACK, HALF], F32, name="rb%d%d" % (cb, h))
 
-        nc.vector.memset(s2_raw[:].bitcast(I32), 0)
         nc.gpsimd.memset(w3s[:].bitcast(I32), 0)
 
         planes = {}
@@ -87,38 +84,52 @@ def tile_list_neighbour_shape_contrast_kernel(
             with nc.allow_non_contiguous_dma(reason="one bias value to a partition"):
                 nc.sync.dma_start(bias[:], b3.rearrange("(c p) -> p c", p=P))
 
-        for a in range(2):
-            nc.sync.dma_start(w2_raw[:, a, :].bitcast(I32), w2_words[a].bitcast(I32))
+        raw = {}
+
+        def load_w2(a):
+            if "w" not in raw:
+                raw["w"] = inter.tile([P, 2, 2 * H], U8, name="w2_raw", tag="woven", align_bytes=64)
+            nc.sync.dma_start(raw["w"][:, a, :].bitcast(I32), w2_words[a].bitcast(I32))
+
+        def load_s2():
+            raw["s"] = inter.tile([P, 2, H], U8, name="s2_raw", tag="woven", align_bytes=64)
+            nc.vector.memset(raw["s"][:].bitcast(I32), 0)
+            for q in range(4):
+                nc.sync.dma_start(
+                    raw["s"][32 * q : 32 * q + 4, :, :].bitcast(I32),
+                    w2_scales[:, 4 * q : 4 * q + 4, :].rearrange("a q c -> q a c").bitcast(I32),
+                )
+
+        load_w2(0)
+        load_w2(1)
+        load_s2()
         load_wg(0)
-        for q in range(4):
-            nc.sync.dma_start(
-                s2_raw[32 * q : 32 * q + 4, :, :].bitcast(I32),
-                w2_scales[:, 4 * q : 4 * q + 4, :].rearrange("a q c -> q a c").bitcast(I32),
-            )
         load_x(0, 0)
         load_wg(1)
-        load_x(0, 1)
         load_x(0, 2)
         load_x(0, 3)
-        load_x(1, 0)
         load_x(1, 1)
+        load_x(0, 1)
         load_x(1, 2)
-        load_w1(0, 0)
+        load_x(1, 0)
         load_x(1, 3)
+        load_w1(0, 0)
         load_w1(0, 1)
-        load_w1(1, 0)
         load_w1(1, 1)
+        load_w1(1, 0)
         load_w3()
 
-        for a in range(2):
+        def perm_w(a):
             nc.vector.tensor_copy(
                 w2c[:, a, :].bitcast(U16).rearrange("p (b t m) -> p b t m", b=2, t=PACK),
-                w2_raw[:, a, :].bitcast(U16).rearrange("p (b m t) -> p b t m", b=2, t=PACK),
+                raw["w"][:, a, :].bitcast(U16).rearrange("p (b m t) -> p b t m", b=2, t=PACK),
             )
-        nc.vector.tensor_copy(
-            w2s[:].rearrange("p a (b t m) -> p (a b) t m", b=2, t=PACK),
-            s2_raw[:].rearrange("p a (b m t) -> p (a b) t m", b=2, t=PACK),
-        )
+
+        def perm_s():
+            nc.vector.tensor_copy(
+                w2s[:].rearrange("p a (b t m) -> p (a b) t m", b=2, t=PACK),
+                raw["s"][:].rearrange("p a (b m t) -> p (a b) t m", b=2, t=PACK),
+            )
 
         def cast(dst, src, eng):
             if eng == "G":
@@ -237,150 +248,158 @@ def tile_list_neighbour_shape_contrast_kernel(
                 hc[:, cb, cols].bitcast(FP8X4), hs[:, cb, cols], hb[cb, j0][:].rearrange("p c t -> p (c t)")
             )
 
-        def y_chunk(j0, width, on_vector):
+        def y_one(j0, width, c, on_vector):
             cols = slice(j0, j0 + width)
-            for c in range(N // P):
-                res = ring.tile([P, width], F32, name="res", tag="res")
-                bank = psum.tile([P, width], F32, name="bank", tag="bank")
-                for cb in range(2):
-                    nc.tensor.matmul_mx(
-                        bank[:],
-                        lhsT=w3c[:, cb, c * P : (c + 1) * P].bitcast(FP8X4),
-                        lhsT_scale=w3s[:, cb, c * P : (c + 1) * P],
-                        rhs=hc[:, cb, cols].bitcast(FP8X4),
-                        rhs_scale=hs[:, cb, cols],
-                        start=(cb == 0),
-                        stop=(cb == 1),
-                    )
-                if c in on_vector:
-                    nc.vector.tensor_scalar(res[:], bank[:], bias[:, c : c + 1], None, ALU.add)
-                else:
-                    nc.scalar.activation(res[:], bank[:], ACT.Identity, bias=bias[:, c : c + 1])
-                nc.sync.dma_start(out[c * P : (c + 1) * P, cols], res[:])
+            res = keep.tile([P, width], F32, name="res%d_%d" % (j0, c))
+            bank = psum.tile([P, width], F32, name="bank", tag="bank")
+            for cb in range(2):
+                nc.tensor.matmul_mx(
+                    bank[:],
+                    lhsT=w3c[:, cb, c * P : (c + 1) * P].bitcast(FP8X4),
+                    lhsT_scale=w3s[:, cb, c * P : (c + 1) * P],
+                    rhs=hc[:, cb, cols].bitcast(FP8X4),
+                    rhs_scale=hs[:, cb, cols],
+                    start=(cb == 0),
+                    stop=(cb == 1),
+                )
+            if on_vector:
+                nc.vector.tensor_scalar(res[:], bank[:], bias[:, c : c + 1], None, ALU.add)
+            else:
+                nc.scalar.activation(res[:], bank[:], ACT.Identity, bias=bias[:, c : c + 1])
+            nc.sync.dma_start(out[c * P : (c + 1) * P, cols], res[:])
 
         gather(0, 0, 0, 0, 512)
+        perm_w(0)
         gather(0, 0, 1, 0, 512)
-        gather(0, 1, 0, 0, 512)
-        gather(0, 1, 1, 0, 512)
-        gather(0, 2, 0, 0, 512)
-        gather(0, 2, 1, 0, 512)
-        gather(0, 3, 0, 0, 512)
         gather(0, 3, 1, 0, 512)
-        weave_x(0, 0, 0, 512, False)
-        weave_x(0, 1, 0, 512, False)
+        gather(1, 1, 0, 0, 512)
+        gather(0, 3, 0, 0, 512)
+        gather(0, 2, 1, 0, 512)
+        gather(1, 1, 1, 0, 512)
+        gather(0, 1, 1, 0, 512)
+        gather(1, 2, 0, 0, 512)
+        gather(0, 2, 0, 0, 512)
         gather(1, 0, 0, 0, 512)
         gather(1, 0, 1, 0, 512)
-        gather(1, 1, 0, 0, 512)
-        gather(1, 1, 1, 0, 512)
-        gather(1, 2, 0, 0, 512)
-        gather(1, 2, 1, 0, 512)
-        weave_w1(0, 0, False, 0, 64)
-        weave_w1(0, 0, False, 64, 128)
-        quant_x(0, 0)
-        b_pass(0, 0, 0, 0)
-        b_pass(0, 0, 1, 0)
-        b_pass(0, 0, 2, 0)
-        b_pass(0, 0, 3, 0)
-        b_pass(1, 0, 0, 0)
-        b_pass(1, 0, 1, 0)
-        b_pass(1, 0, 2, 0)
-        b_pass(1, 0, 3, 0)
+        gather(0, 1, 0, 0, 512)
         gather(1, 3, 0, 0, 256)
-        weave_x(1, 0, 0, 256, False)
-        gather(1, 3, 0, 256, 512)
-        weave_x(1, 0, 256, 512, True)
+        weave_x(0, 1, 0, 512, False)
+        weave_x(0, 0, 0, 512, False)
+        quant_x(0, 0)
+        weave_w1(0, 0, True, 0, 64)
         gather(1, 3, 1, 0, 512)
-        quant_x(0, 1)
-        quant_x(1, 0)
-        b_pass(0, 0, 0, 1)
-        b_pass(0, 0, 1, 1)
-        b_pass(0, 0, 2, 1)
-        b_pass(0, 0, 3, 1)
-        b_pass(1, 0, 0, 1)
-        b_pass(1, 0, 1, 1)
-        b_pass(1, 0, 2, 1)
-        b_pass(1, 0, 3, 1)
-        weave_x(1, 1, 0, 256, True)
-        weave_x(1, 1, 256, 512, True)
-        quant_w1(0, 0)
-        quant_x(1, 1)
-        relu_b(0, 0, 0, True)
-        relu_b(0, 0, 1, False)
-        relu_b(0, 0, 2, False)
-        relu_b(0, 0, 3, False)
+        perm_s()
+        weave_w1(0, 0, False, 64, 128)
+        gather(1, 3, 0, 256, 512)
+        gather(1, 2, 1, 0, 512)
+        weave_x(1, 0, 0, 256, False)
         weave_w1(0, 1, False, 0, 64)
-        weave_w1(0, 1, True, 64, 128)
-        quant_w1(0, 1)
+        b_pass(1, 0, 2, 0)
+        weave_x(1, 0, 256, 512, True)
+        perm_w(1)
+        b_pass(1, 0, 0, 0)
+        quant_x(1, 0)
+        b_pass(0, 0, 0, 0)
+        b_pass(0, 0, 2, 0)
+        b_pass(0, 0, 0, 1)
+        b_pass(1, 0, 2, 1)
+        weave_x(1, 1, 256, 512, True)
+        b_pass(0, 0, 1, 0)
+        b_pass(0, 0, 3, 0)
+        quant_x(0, 1)
+        b_pass(1, 0, 0, 1)
+        b_pass(1, 0, 3, 0)
+        b_pass(0, 0, 2, 1)
+        weave_x(1, 1, 0, 256, False)
+        b_pass(0, 1, 2, 0)
+        quant_x(1, 1)
         b_pass(0, 1, 0, 0)
         b_pass(0, 1, 0, 1)
-        b_pass(0, 1, 1, 0)
-        b_pass(0, 1, 1, 1)
-        b_pass(0, 1, 2, 0)
-        b_pass(0, 1, 2, 1)
-        b_pass(0, 1, 3, 0)
-        b_pass(0, 1, 3, 1)
-        relu_b(1, 0, 0, False)
-        relu_b(1, 0, 1, False)
         relu_b(1, 0, 2, False)
-        relu_b(1, 0, 3, False)
-        a_mm(0, 0, 256)
-        sub(0, 0, 256)
-        absw(0, 0, 0, 256)
-        a_mm(0, 256, 256)
-        sub(0, 256, 256)
-        absw(0, 256, 0, 256)
-        relu_b(0, 1, 0, False)
-        relu_b(0, 1, 1, True)
-        relu_b(0, 1, 2, False)
-        relu_b(0, 1, 3, True)
-        weave_w1(1, 0, True, 0, 64)
-        weave_w1(1, 0, False, 64, 128)
+        weave_w1(0, 1, True, 64, 128)
+        b_pass(0, 0, 1, 1)
+        relu_b(0, 0, 0, False)
+        b_pass(0, 1, 3, 0)
+        relu_b(1, 0, 0, True)
         weave_w1(1, 1, True, 0, 64)
+        quant_w1(0, 0)
+        b_pass(1, 0, 3, 1)
+        quant_w1(0, 1)
         weave_w1(1, 1, False, 64, 128)
-        b_pass(1, 1, 0, 0)
-        b_pass(1, 1, 0, 1)
-        b_pass(1, 1, 1, 0)
-        b_pass(1, 1, 1, 1)
-        b_pass(1, 1, 2, 0)
-        b_pass(1, 1, 2, 1)
-        b_pass(1, 1, 3, 0)
-        b_pass(1, 1, 3, 1)
-        quant_h(0, 0, 256)
-        quant_w1(1, 0)
+        b_pass(1, 0, 1, 0)
+        relu_b(0, 0, 1, True)
         quant_w1(1, 1)
-        quant_h(0, 256, 256)
+        a_mm(0, 0, 256)
+        relu_b(0, 0, 2, False)
+        b_pass(1, 1, 1, 0)
+        b_pass(0, 1, 1, 0)
+        relu_b(1, 0, 3, True)
+        b_pass(0, 0, 3, 1)
+        a_mm(0, 256, 256)
+        b_pass(0, 1, 2, 1)
+        b_pass(1, 1, 0, 0)
+        relu_b(0, 0, 3, False)
+        b_pass(0, 1, 1, 1)
         a_mm(0, 512, 256)
+        sub(0, 0, 256)
+        sub(0, 256, 256)
+        b_pass(1, 1, 3, 0)
+        weave_w1(1, 0, True, 64, 128)
+        b_pass(1, 0, 1, 1)
+        b_pass(0, 1, 3, 1)
+        b_pass(1, 1, 1, 1)
+        weave_w1(1, 0, True, 0, 64)
+        relu_b(0, 1, 1, False)
+        absw(0, 0, 0, 256)
+        b_pass(1, 1, 2, 0)
+        relu_b(0, 1, 0, False)
+        quant_h(0, 0, 256)
+        b_pass(1, 1, 3, 1)
+        b_pass(1, 1, 2, 1)
+        relu_b(0, 1, 2, False)
+        relu_b(0, 1, 3, False)
+        absw(0, 256, 0, 256)
+        quant_w1(1, 0)
+        relu_b(1, 0, 1, False)
         sub(0, 512, 256)
+        relu_b(1, 1, 3, False)
+        a_mm(1, 256, 256)
+        quant_h(0, 256, 256)
+        b_pass(1, 1, 0, 1)
         absw(0, 512, 0, 256)
         a_mm(0, 768, 256)
-        sub(0, 768, 256)
-        absw(0, 768, 0, 256)
-        relu_b(1, 1, 0, False)
-        relu_b(1, 1, 1, False)
-        relu_b(1, 1, 2, False)
-        relu_b(1, 1, 3, False)
         a_mm(1, 0, 256)
-        sub(1, 0, 256)
-        absw(1, 0, 0, 256)
-        quant_h(0, 512, 256)
-        a_mm(1, 256, 256)
         sub(1, 256, 256)
-        absw(1, 256, 0, 256)
-        quant_h(0, 768, 256)
-        quant_h(1, 0, 256)
+        sub(0, 768, 256)
         a_mm(1, 512, 256)
+        relu_b(1, 1, 1, False)
+        sub(1, 0, 256)
+        absw(1, 256, 0, 256)
+        a_mm(1, 896, 128)
+        quant_h(0, 512, 256)
+        relu_b(1, 1, 2, False)
+        relu_b(1, 1, 0, False)
         sub(1, 512, 256)
+        sub(1, 896, 128)
+        a_mm(1, 768, 128)
+        absw(0, 768, 0, 256)
+        absw(1, 0, 0, 256)
         absw(1, 512, 0, 256)
         quant_h(1, 256, 256)
-        y_chunk(0, 512, (0, 2))
-        a_mm(1, 768, 128)
+        quant_h(1, 0, 256)
+        y_one(0, 512, 0, False)
+        quant_h(0, 768, 256)
         sub(1, 768, 128)
-        absw(1, 768, 0, 128)
         quant_h(1, 512, 256)
-        a_mm(1, 896, 128)
-        sub(1, 896, 128)
         absw(1, 896, 0, 128)
-        y_chunk(512, 256, (0, 2))
-        quant_h(1, 768, 128)
+        y_one(0, 512, 2, False)
+        y_one(0, 512, 1, True)
+        absw(1, 768, 0, 128)
+        y_one(512, 256, 0, False)
+        y_one(512, 256, 1, True)
         quant_h(1, 896, 128)
-        y_chunk(768, 256, (0, 2))
+        quant_h(1, 768, 128)
+        y_one(512, 256, 2, False)
+        y_one(768, 256, 2, False)
+        y_one(768, 256, 0, True)
+        y_one(768, 256, 1, False)

@@ -20,6 +20,9 @@ P = 128
 PACK = 4
 KP = P * PACK
 HALF = 512
+UNIT = 256
+RUN = 4
+HOLD = 768
 
 
 def tile_list_neighbour_shape_contrast_kernel(
@@ -28,32 +31,42 @@ def tile_list_neighbour_shape_contrast_kernel(
     nc = tc.nc
     with ExitStack() as ctx:
         keep = ctx.enter_context(tc.tile_pool(name="keep", bufs=1))
-        stream = ctx.enter_context(tc.tile_pool(name="stream", bufs=10))
-        gath = ctx.enter_context(tc.tile_pool(name="gath", bufs=4))
-        inter = ctx.enter_context(tc.tile_pool(name="inter", bufs=7))
+        stream = ctx.enter_context(tc.tile_pool(name="stream", bufs=8))
+        wide = ctx.enter_context(tc.tile_pool(name="wide", bufs=5))
         ring = ctx.enter_context(tc.tile_pool(name="ring", bufs=4))
         psum = ctx.enter_context(tc.psum_pool(name="psum", bufs=8))
 
         offsets = keep.tile([P, S // 16], U16, name="offsets")
         nc.sync.dma_start(offsets[:], offs)
 
+        def mx_tiles(name, shape):
+            codes = keep.tile(shape, U32, name=name + "_codes", align_bytes=64)
+            scales = keep.tile(shape, U8, name=name + "_scales", align_bytes=64)
+            return codes, scales
+
+        w2_raw = keep.tile([P, 2, 2 * H], U8, name="w2_raw", align_bytes=64)
+        s2_raw = keep.tile([P, 2, H], U8, name="s2_raw", align_bytes=64)
         w2c = keep.tile([P, 2, 2 * H], U8, name="w2c", align_bytes=64)
         w2s = keep.tile([P, 2, H], U8, name="w2s", align_bytes=64)
-        w3c = keep.tile([P, 2, N], U32, name="w3c", align_bytes=64)
-        w3s = keep.tile([P, 2, N], U8, name="w3s", align_bytes=64)
+        w3c, w3s = mx_tiles("w3", [P, 2, N])
         bias = keep.tile([P, N // P], F32, name="bias")
-        wg = [keep.tile([P, HALF], F32, name="wg%d" % h) for h in range(2)]
-        xc = keep.tile([P, 2, S], U32, name="xc", align_bytes=64)
-        xs = keep.tile([P, 2, S], U8, name="xs", align_bytes=64)
-        w1c = keep.tile([P, 2, H], U32, name="w1c", align_bytes=64)
-        w1s = keep.tile([P, 2, H], U8, name="w1s", align_bytes=64)
-        hc = keep.tile([P, 2, S], U32, name="hc", align_bytes=64)
-        hs = keep.tile([P, 2, S], U8, name="hs", align_bytes=64)
-        rb = {}
+        late = keep.tile([P, (PACK + 1) * HALF], F32, name="late", align_bytes=64)
+        wg = [late[:, HOLD : HOLD + HALF], keep.tile([P, HALF], F32, name="wg1")[:]]
+        xq = [mx_tiles("x%d" % h, [P, 2, HALF]) for h in range(2)]
+        xb00 = keep.tile([P, HALF * PACK], BF16, name="xb00", align_bytes=64)
+        xb1 = keep.tile([P, 2 * HALF * PACK], BF16, name="xb1", align_bytes=64)
+        xb = {(0, 0): xb00[:], (1, 0): late[:, 3 * HALF :].bitcast(BF16)}
+        for a in range(2):
+            xb[a, 1] = xb1[:, a * HALF * PACK : (a + 1) * HALF * PACK]
+        w1q = {}
+        wb = {}
         for cb in range(2):
-            for h in range(2):
-                rb[cb, h] = keep.tile([P, PACK, HALF], F32, name="rb%d%d" % (cb, h))
+            for tp in range(2):
+                w1q[cb, tp] = mx_tiles("w1_%d%d" % (cb, tp), [P, 2, 2 * P])
+                wb[cb, tp] = keep.tile([P, 2, 2, P, PACK], BF16, name="wb%d%d" % (cb, tp), align_bytes=64)
+        hq = [mx_tiles("h%d" % cb, [P, S]) for cb in range(2)]
 
+        nc.gpsimd.memset(s2_raw[:].bitcast(I32), 0)
         nc.gpsimd.memset(w3s[:].bitcast(I32), 0)
 
         planes = {}
@@ -72,334 +85,258 @@ def tile_list_neighbour_shape_contrast_kernel(
             )
 
         def load_wg(h):
-            nc.sync.dma_start(wg[h][:], wgt[:, h * HALF : (h + 1) * HALF])
+            nc.sync.dma_start(wg[h], wgt[:, h * HALF : (h + 1) * HALF])
+
+        def load_scales(dst, src):
+            for q in range(4):
+                nc.sync.dma_start(
+                    dst[32 * q : 32 * q + 4, :, :].bitcast(I32),
+                    src[:, 4 * q : 4 * q + 4, :].rearrange("a q c -> q a c").bitcast(I32),
+                )
+
+        def load_w2():
+            nc.sync.dma_start(w2_raw[:].bitcast(I32), w2_words.rearrange("a p c -> p a c").bitcast(I32))
 
         def load_w3():
             nc.sync.dma_start(w3c[:].bitcast(I32), w3_words.rearrange("a p c i -> p a (c i)").bitcast(I32))
-            for q in range(4):
-                nc.sync.dma_start(
-                    w3s[32 * q : 32 * q + 4, :, :].bitcast(I32),
-                    w3_scales[:, 4 * q : 4 * q + 4, :].rearrange("a q c -> q a c").bitcast(I32),
-                )
+            load_scales(w3s, w3_scales)
             with nc.allow_non_contiguous_dma(reason="one bias value to a partition"):
                 nc.sync.dma_start(bias[:], b3.rearrange("(c p) -> p c", p=P))
 
-        raw = {}
-
-        def load_w2(a):
-            if "w" not in raw:
-                raw["w"] = inter.tile([P, 2, 2 * H], U8, name="w2_raw", tag="woven", align_bytes=64)
-            nc.sync.dma_start(raw["w"][:, a, :].bitcast(I32), w2_words[a].bitcast(I32))
-
-        def load_s2():
-            raw["s"] = inter.tile([P, 2, H], U8, name="s2_raw", tag="woven", align_bytes=64)
-            nc.vector.memset(raw["s"][:].bitcast(I32), 0)
-            for q in range(4):
-                nc.sync.dma_start(
-                    raw["s"][32 * q : 32 * q + 4, :, :].bitcast(I32),
-                    w2_scales[:, 4 * q : 4 * q + 4, :].rearrange("a q c -> q a c").bitcast(I32),
-                )
-
-        load_w2(0)
-        load_w2(1)
-        load_s2()
-        load_wg(0)
-        load_x(0, 0)
-        load_wg(1)
-        load_x(0, 2)
-        load_x(0, 3)
-        load_x(1, 1)
-        load_x(0, 1)
-        load_x(1, 2)
-        load_x(1, 0)
-        load_x(1, 3)
-        load_w1(0, 0)
-        load_w1(0, 1)
-        load_w1(1, 1)
-        load_w1(1, 0)
-        load_w3()
-
-        def perm_w(a):
+        def deal_w2_words():
             nc.vector.tensor_copy(
-                w2c[:, a, :].bitcast(U16).rearrange("p (b t m) -> p b t m", b=2, t=PACK),
-                raw["w"][:, a, :].bitcast(U16).rearrange("p (b m t) -> p b t m", b=2, t=PACK),
+                w2c[:].bitcast(U16).rearrange("p a (b t m) -> p (a b) t m", b=2, t=PACK),
+                w2_raw[:].bitcast(U16).rearrange("p a (b m t) -> p (a b) t m", b=2, t=PACK),
             )
 
-        def perm_s():
+        def deal_w2_scales():
             nc.vector.tensor_copy(
                 w2s[:].rearrange("p a (b t m) -> p (a b) t m", b=2, t=PACK),
-                raw["s"][:].rearrange("p a (b m t) -> p (a b) t m", b=2, t=PACK),
+                s2_raw[:].rearrange("p a (b m t) -> p (a b) t m", b=2, t=PACK),
             )
 
-        def cast(dst, src, eng):
-            if eng == "G":
-                nc.gpsimd.tensor_scalar(dst, src, 1.0, 0.0, ALU.mult, ALU.add)
-            elif eng:
-                nc.vector.tensor_copy(dst, src)
-            else:
+        def cast(eng, dst, src):
+            if eng is nc.scalar:
                 nc.scalar.copy(dst, src)
+            elif eng is nc.gpsimd:
+                nc.gpsimd.tensor_scalar(dst, src, 1.0, 0.0, ALU.mult, ALU.add)
+            else:
+                nc.vector.tensor_copy(dst, src)
 
         g4 = {}
-        xb = {}
 
-        def gather(a, i, h, lo, hi):
-            if (a, h) not in g4:
-                g4[a, h] = gath.tile([P, PACK, HALF], F32, name="g4")
+        def gather(a, i, h):
+            if (a, i, h) == (1, 0, 1):
+                g4[a, h] = late[:, : PACK * HALF].rearrange("p (t c) -> p t c", t=PACK)
+            elif i == 0:
+                g4[a, h] = wide.tile([P, PACK, HALF], F32, name="g4", tag="wide")[:]
             j0 = h * HALF
             nc.vector.tensor_tensor(
-                g4[a, h][:, i, lo:hi],
-                planes[a, i][:].indirect(offsets[:, (j0 + lo) // 16 : (j0 + hi) // 16]),
-                wg[h][:, lo:hi],
+                g4[a, h][:, i, :],
+                planes[a, i][:].indirect(offsets[:, j0 // 16 : (j0 + HALF) // 16]),
+                wg[h],
                 ALU.mult,
             )
 
-        def weave_x(a, h, lo, hi, eng):
-            if (a, h) not in xb:
-                xb[a, h] = inter.tile([P, HALF, PACK], BF16, name="xb", tag="woven", align_bytes=64)
-            dst = xb[a, h][:, lo:hi, :].rearrange("p (c i) t -> p c t i", i=4)
-            src = g4[a, h][:, :, lo:hi].rearrange("p t (c i) -> p c t i", i=4)
-            cast(dst, src, eng)
+        def weave_x(eng, a, h):
+            dst = xb[a, h].rearrange("p (c i t) -> p c t i", i=RUN, t=PACK)
+            src = g4[a, h].rearrange("p t (c i) -> p c t i", i=RUN)
+            cast(eng, dst, src)
 
-        def quant_x(a, h):
-            cols = slice(h * HALF, (h + 1) * HALF)
+        def quant_x(h, passes, src):
+            codes, scales = xq[h]
             nc.vector.quantize_mx(
-                xc[:, a, cols].bitcast(FP8X4), xs[:, a, cols], xb[a, h][:].rearrange("p c t -> p (c t)")
+                codes[:, passes, :].rearrange("p a c -> p (a c)").bitcast(FP8X4),
+                scales[:, passes, :].rearrange("p a c -> p (a c)"),
+                src,
             )
 
-        wb = {}
+        def weave_w1(eng, cb, a, tp):
+            dst = wb[cb, tp][:, a, :, :, :].rearrange("p t m j -> p m j t")
+            src = w1_raw[cb, a][:].rearrange("p j (m t) -> p m j t", t=PACK)[:, :, :, 2 * tp : 2 * tp + 2]
+            cast(eng, dst, src)
 
-        def weave_w1(cb, a, eng, lo, hi):
-            if (cb, a) not in wb:
-                wb[cb, a] = inter.tile([P, PACK, P, PACK], BF16, name="wb", tag="woven", align_bytes=64)
-            t0 = lo // 32
-            dst = wb[cb, a][:, t0 : t0 + 2, :, :].rearrange("p t m j -> p m j t")
-            src = w1_raw[cb, a][:].rearrange("p j (m t) -> p m j t", t=PACK)[:, :, :, t0 : t0 + 2]
-            cast(dst, src, eng)
-
-        def quant_w1(cb, a):
-            cols = slice(cb * KP, (cb + 1) * KP)
+        def quant_w1(cb, tp):
+            codes, scales = w1q[cb, tp]
             nc.vector.quantize_mx(
-                w1c[:, a, cols].bitcast(FP8X4), w1s[:, a, cols], wb[cb, a][:].rearrange("p t m j -> p (t m j)")
+                codes[:].rearrange("p a c -> p (a c)").bitcast(FP8X4),
+                scales[:].rearrange("p a c -> p (a c)"),
+                wb[cb, tp][:].rearrange("p a t m j -> p (a t m j)"),
             )
 
         bbank = {}
+        rb = {}
 
         def b_pass(cb, h, t, a):
             if a == 0:
                 bbank[cb, h, t] = psum.tile([P, HALF], F32, name="bank", tag="bank")
             c0 = cb * KP + t * P
-            cols = slice(h * HALF, (h + 1) * HALF)
+            codes, scales = xq[h]
             nc.tensor.matmul_mx(
                 bbank[cb, h, t][:],
                 lhsT=w2c[:, a, 2 * c0 : 2 * (c0 + P)].bitcast(FP4X4),
                 lhsT_scale=w2s[:, a, c0 : c0 + P],
-                rhs=xc[:, a, cols].bitcast(FP8X4),
-                rhs_scale=xs[:, a, cols],
+                rhs=codes[:, a, :].bitcast(FP8X4),
+                rhs_scale=scales[:, a, :],
                 start=(a == 0),
                 stop=(a == 1),
             )
 
-        def relu_b(cb, h, t, eng):
-            if eng:
-                nc.vector.tensor_scalar(rb[cb, h][:, t, :], bbank[cb, h, t][:], 0.0, None, ALU.max)
-            else:
+        def relu_b(eng, cb, h, t):
+            if (cb, h) not in rb:
+                rb[cb, h] = wide.tile([P, PACK, HALF], F32, name="rb", tag="wide")
+            if eng is nc.scalar:
                 nc.scalar.activation(rb[cb, h][:, t, :], bbank[cb, h, t][:], ACT.Relu)
+            else:
+                nc.vector.tensor_scalar(rb[cb, h][:, t, :], bbank[cb, h, t][:], 0.0, None, ALU.max)
 
-        abank = {}
+        def b_tile(eng, cb, h, t):
+            b_pass(cb, h, t, 0)
+            b_pass(cb, h, t, 1)
+            relu_b(eng, cb, h, t)
+
+        def a_sub(cb, j0, w):
+            per = HALF // w
+            h, jl = divmod(j0, HALF)
+            xcodes, xscales = xq[h]
+            for u in range(PACK // per):
+                bank = psum.tile([P, per, w], F32, name="bank", tag="bank")
+                for v in range(per):
+                    tp, tt = divmod(u * per + v, 2)
+                    codes, scales = w1q[cb, tp]
+                    for a in range(2):
+                        nc.tensor.matmul_mx(
+                            bank[:, v, :],
+                            lhsT=codes[:, a, tt * P : (tt + 1) * P].bitcast(FP8X4),
+                            lhsT_scale=scales[:, a, tt * P : (tt + 1) * P],
+                            rhs=xcodes[:, a, jl : jl + w].bitcast(FP8X4),
+                            rhs_scale=xscales[:, a, jl : jl + w],
+                            start=(a == 0),
+                            stop=(a == 1),
+                        )
+                part = rb[cb, h][:, u * per : (u + 1) * per, jl : jl + w]
+                nc.vector.tensor_tensor(part, bank[:], part, ALU.subtract)
+
         hb = {}
 
-        def a_mm(cb, j0, w):
-            per = HALF // w
-            cols = slice(j0, j0 + w)
-            for t in range(PACK):
-                if t % per == 0:
-                    abank[cb, j0, t // per] = psum.tile([P, per, w], F32, name="bank", tag="bank")
-                c0 = cb * KP + t * P
-                for a in range(2):
-                    nc.tensor.matmul_mx(
-                        abank[cb, j0, t // per][:, t % per, :],
-                        lhsT=w1c[:, a, c0 : c0 + P].bitcast(FP8X4),
-                        lhsT_scale=w1s[:, a, c0 : c0 + P],
-                        rhs=xc[:, a, cols].bitcast(FP8X4),
-                        rhs_scale=xs[:, a, cols],
-                        start=(a == 0),
-                        stop=(a == 1),
-                    )
-
-        def sub(cb, j0, w):
-            per = HALF // w
-            jl = j0 % HALF
-            for u in range(PACK // per):
-                part = rb[cb, j0 // HALF][:, u * per : (u + 1) * per, jl : jl + w]
-                nc.vector.tensor_tensor(part, abank[cb, j0, u][:], part, ALU.subtract)
-
-        def absw(cb, j0, lo, hi):
-            jl = j0 % HALF
-            hb[cb, j0] = ring.tile([P, hi, PACK], BF16, name="hb", tag="hb", align_bytes=64)
+        def abs_h(cb, j0, w):
+            h, jl = divmod(j0, HALF)
+            hb[cb, j0] = ring.tile([P, w, PACK], BF16, name="hb", tag="hb", align_bytes=64)
             nc.scalar.activation(
-                hb[cb, j0][:].rearrange("p (c i) t -> p c t i", i=4),
-                rb[cb, j0 // HALF][:, :, jl : jl + hi].rearrange("p t (c i) -> p c t i", i=4),
+                hb[cb, j0][:].rearrange("p (c i) t -> p c t i", i=RUN),
+                rb[cb, h][:, :, jl : jl + w].rearrange("p t (c i) -> p c t i", i=RUN),
                 ACT.Abs,
             )
 
         def quant_h(cb, j0, w):
-            cols = slice(j0, j0 + w)
+            codes, scales = hq[cb]
             nc.vector.quantize_mx(
-                hc[:, cb, cols].bitcast(FP8X4), hs[:, cb, cols], hb[cb, j0][:].rearrange("p c t -> p (c t)")
+                codes[:, j0 : j0 + w].bitcast(FP8X4),
+                scales[:, j0 : j0 + w],
+                hb[cb, j0][:].rearrange("p c t -> p (c t)"),
             )
 
-        def y_one(j0, width, c, on_vector):
-            cols = slice(j0, j0 + width)
-            res = keep.tile([P, width], F32, name="res%d_%d" % (j0, c))
-            bank = psum.tile([P, width], F32, name="bank", tag="bank")
+        def y_tile(eng, j0, w, c):
+            cols = slice(j0, j0 + w)
+            res = keep.tile([P, w], F32, name="res%d_%d" % (j0, c))
+            bank = psum.tile([P, w], F32, name="bank", tag="bank")
             for cb in range(2):
+                codes, scales = hq[cb]
                 nc.tensor.matmul_mx(
                     bank[:],
                     lhsT=w3c[:, cb, c * P : (c + 1) * P].bitcast(FP8X4),
                     lhsT_scale=w3s[:, cb, c * P : (c + 1) * P],
-                    rhs=hc[:, cb, cols].bitcast(FP8X4),
-                    rhs_scale=hs[:, cb, cols],
+                    rhs=codes[:, cols].bitcast(FP8X4),
+                    rhs_scale=scales[:, cols],
                     start=(cb == 0),
                     stop=(cb == 1),
                 )
-            if on_vector:
-                nc.vector.tensor_scalar(res[:], bank[:], bias[:, c : c + 1], None, ALU.add)
-            else:
+            if eng is nc.scalar:
                 nc.scalar.activation(res[:], bank[:], ACT.Identity, bias=bias[:, c : c + 1])
+            else:
+                nc.vector.tensor_scalar(res[:], bank[:], bias[:, c : c + 1], None, ALU.add)
             nc.sync.dma_start(out[c * P : (c + 1) * P, cols], res[:])
 
-        gather(0, 0, 0, 0, 512)
-        perm_w(0)
-        gather(0, 0, 1, 0, 512)
-        gather(0, 3, 1, 0, 512)
-        gather(1, 1, 0, 0, 512)
-        gather(0, 3, 0, 0, 512)
-        gather(0, 2, 1, 0, 512)
-        gather(1, 1, 1, 0, 512)
-        gather(0, 1, 1, 0, 512)
-        gather(1, 2, 0, 0, 512)
-        gather(0, 2, 0, 0, 512)
-        gather(1, 0, 0, 0, 512)
-        gather(1, 0, 1, 0, 512)
-        gather(0, 1, 0, 0, 512)
-        gather(1, 3, 0, 0, 256)
-        weave_x(0, 1, 0, 512, False)
-        weave_x(0, 0, 0, 512, False)
-        quant_x(0, 0)
-        weave_w1(0, 0, True, 0, 64)
-        gather(1, 3, 1, 0, 512)
-        perm_s()
-        weave_w1(0, 0, False, 64, 128)
-        gather(1, 3, 0, 256, 512)
-        gather(1, 2, 1, 0, 512)
-        weave_x(1, 0, 0, 256, False)
-        weave_w1(0, 1, False, 0, 64)
-        b_pass(1, 0, 2, 0)
-        weave_x(1, 0, 256, 512, True)
-        perm_w(1)
-        b_pass(1, 0, 0, 0)
-        quant_x(1, 0)
-        b_pass(0, 0, 0, 0)
-        b_pass(0, 0, 2, 0)
-        b_pass(0, 0, 0, 1)
-        b_pass(1, 0, 2, 1)
-        weave_x(1, 1, 256, 512, True)
-        b_pass(0, 0, 1, 0)
-        b_pass(0, 0, 3, 0)
-        quant_x(0, 1)
-        b_pass(1, 0, 0, 1)
-        b_pass(1, 0, 3, 0)
-        b_pass(0, 0, 2, 1)
-        weave_x(1, 1, 0, 256, False)
-        b_pass(0, 1, 2, 0)
-        quant_x(1, 1)
-        b_pass(0, 1, 0, 0)
-        b_pass(0, 1, 0, 1)
-        relu_b(1, 0, 2, False)
-        weave_w1(0, 1, True, 64, 128)
-        b_pass(0, 0, 1, 1)
-        relu_b(0, 0, 0, False)
-        b_pass(0, 1, 3, 0)
-        relu_b(1, 0, 0, True)
-        weave_w1(1, 1, True, 0, 64)
-        quant_w1(0, 0)
-        b_pass(1, 0, 3, 1)
-        quant_w1(0, 1)
-        weave_w1(1, 1, False, 64, 128)
-        b_pass(1, 0, 1, 0)
-        relu_b(0, 0, 1, True)
-        quant_w1(1, 1)
-        a_mm(0, 0, 256)
-        relu_b(0, 0, 2, False)
-        b_pass(1, 1, 1, 0)
-        b_pass(0, 1, 1, 0)
-        relu_b(1, 0, 3, True)
-        b_pass(0, 0, 3, 1)
-        a_mm(0, 256, 256)
-        b_pass(0, 1, 2, 1)
-        b_pass(1, 1, 0, 0)
-        relu_b(0, 0, 3, False)
-        b_pass(0, 1, 1, 1)
-        a_mm(0, 512, 256)
-        sub(0, 0, 256)
-        sub(0, 256, 256)
-        b_pass(1, 1, 3, 0)
-        weave_w1(1, 0, True, 64, 128)
-        b_pass(1, 0, 1, 1)
-        b_pass(0, 1, 3, 1)
-        b_pass(1, 1, 1, 1)
-        weave_w1(1, 0, True, 0, 64)
-        relu_b(0, 1, 1, False)
-        absw(0, 0, 0, 256)
-        b_pass(1, 1, 2, 0)
-        relu_b(0, 1, 0, False)
-        quant_h(0, 0, 256)
-        b_pass(1, 1, 3, 1)
-        b_pass(1, 1, 2, 1)
-        relu_b(0, 1, 2, False)
-        relu_b(0, 1, 3, False)
-        absw(0, 256, 0, 256)
-        quant_w1(1, 0)
-        relu_b(1, 0, 1, False)
-        sub(0, 512, 256)
-        relu_b(1, 1, 3, False)
-        a_mm(1, 256, 256)
-        quant_h(0, 256, 256)
-        b_pass(1, 1, 0, 1)
-        absw(0, 512, 0, 256)
-        a_mm(0, 768, 256)
-        a_mm(1, 0, 256)
-        sub(1, 256, 256)
-        sub(0, 768, 256)
-        a_mm(1, 512, 256)
-        relu_b(1, 1, 1, False)
-        sub(1, 0, 256)
-        absw(1, 256, 0, 256)
-        a_mm(1, 896, 128)
-        quant_h(0, 512, 256)
-        relu_b(1, 1, 2, False)
-        relu_b(1, 1, 0, False)
-        sub(1, 512, 256)
-        sub(1, 896, 128)
-        a_mm(1, 768, 128)
-        absw(0, 768, 0, 256)
-        absw(1, 0, 0, 256)
-        absw(1, 512, 0, 256)
-        quant_h(1, 256, 256)
-        quant_h(1, 0, 256)
-        y_one(0, 512, 0, False)
-        quant_h(0, 768, 256)
-        sub(1, 768, 128)
-        quant_h(1, 512, 256)
-        absw(1, 896, 0, 128)
-        y_one(0, 512, 2, False)
-        y_one(0, 512, 1, True)
-        absw(1, 768, 0, 128)
-        y_one(512, 256, 0, False)
-        y_one(512, 256, 1, True)
-        quant_h(1, 896, 128)
-        quant_h(1, 768, 128)
-        y_one(512, 256, 2, False)
-        y_one(768, 256, 2, False)
-        y_one(768, 256, 0, True)
-        y_one(768, 256, 1, False)
+        V, A = nc.vector, nc.scalar
+
+        load_scales(s2_raw, w2_scales)
+        load_wg(0)
+        load_x(0, 0)
+        load_wg(1)
+        load_x(0, 1)
+        load_w2()
+        for a in range(2):
+            for i in range(PACK):
+                if (a, i) > (0, 1):
+                    load_x(a, i)
+        for cb in range(2):
+            for a in range(2):
+                load_w1(cb, a)
+        load_w3()
+
+        deal_w2_scales()
+        for i in range(PACK):
+            for h in range(2):
+                gather(0, i, h)
+            if i == 1:
+                deal_w2_words()
+        weave_x(A, 0, 0)
+        weave_x(A, 0, 1)
+        gather(1, 0, 0)
+        gather(1, 0, 1)
+        for i in range(1, PACK):
+            gather(1, i, 0)
+        quant_x(0, slice(0, 1), xb[0, 0])
+        for cb in range(2):
+            for t in range(PACK):
+                b_pass(cb, 0, t, 0)
+        weave_x(A, 1, 0)
+        gather(1, 1, 1)
+        gather(1, 2, 1)
+        quant_x(0, slice(1, 2), xb[1, 0])
+        gather(1, 3, 1)
+        weave_w1(A, 0, 0, 0)
+        weave_w1(A, 0, 0, 1)
+        weave_x(V, 1, 1)
+        quant_x(1, slice(0, 2), xb1[:])
+        for cb in range(2):
+            for t in range(PACK):
+                b_pass(cb, 0, t, 1)
+                relu_b(A, cb, 0, t)
+        for tp in range(2):
+            weave_w1(V, 0, 1, tp)
+        for tp in range(2):
+            quant_w1(0, tp)
+        for t in range(PACK):
+            b_tile(A, 0, 1, t)
+        for tp in range(2):
+            weave_w1(V, 1, 0, tp)
+        a_sub(0, 0, UNIT)
+        abs_h(0, 0, UNIT)
+        for tp in range(2):
+            weave_w1(V, 1, 1, tp)
+        for t in range(2):
+            b_tile(A, 1, 1, t)
+        a_sub(0, UNIT, UNIT)
+        abs_h(0, UNIT, UNIT)
+        for tp in range(2):
+            quant_w1(1, tp)
+        for t in range(2, PACK):
+            b_tile(A, 1, 1, t)
+        steps = [(0, 2 * UNIT, UNIT), (0, 3 * UNIT, UNIT), (1, 0, UNIT), (1, UNIT, UNIT), (1, 2 * UNIT, UNIT)]
+        steps = steps + [(1, 3 * UNIT, P), (1, 3 * UNIT + P, P)]
+        waiting = [(0, 0, UNIT), (0, UNIT, UNIT)]
+        for step in steps:
+            a_sub(*step)
+            abs_h(*step)
+            quant_h(*waiting[0])
+            waiting = waiting[1:] + [step]
+        for step in waiting[:1]:
+            quant_h(*step)
+        for c in range(N // P):
+            y_tile(A if c % 2 == 0 else V, 0, HALF, c)
+        for c in range(N // P):
+            y_tile(A if c % 2 == 0 else V, HALF, UNIT, c)
+        quant_h(*waiting[1])
+        for c in range(N // P):
+            y_tile(V if c % 2 == 0 else A, HALF + UNIT, UNIT, c)

@@ -22,7 +22,7 @@ KP = P * PACK
 HALF = 512
 UNIT = 256
 RUN = 4
-HOLD = 768
+HOLD = 1024
 
 
 def tile_list_neighbour_shape_contrast_kernel(
@@ -31,9 +31,8 @@ def tile_list_neighbour_shape_contrast_kernel(
     nc = tc.nc
     with ExitStack() as ctx:
         keep = ctx.enter_context(tc.tile_pool(name="keep", bufs=1))
-        stream = ctx.enter_context(tc.tile_pool(name="stream", bufs=8))
         wide = ctx.enter_context(tc.tile_pool(name="wide", bufs=5))
-        ring = ctx.enter_context(tc.tile_pool(name="ring", bufs=4))
+        ring = ctx.enter_context(tc.tile_pool(name="ring", bufs=6))
         psum = ctx.enter_context(tc.psum_pool(name="psum", bufs=8))
 
         offsets = keep.tile([P, S // 16], U16, name="offsets")
@@ -50,14 +49,10 @@ def tile_list_neighbour_shape_contrast_kernel(
         w2s = keep.tile([P, 2, H], U8, name="w2s", align_bytes=64)
         w3c, w3s = mx_tiles("w3", [P, 2, N])
         bias = keep.tile([P, N // P], F32, name="bias")
-        late = keep.tile([P, (PACK + 1) * HALF], F32, name="late", align_bytes=64)
+        late = keep.tile([P, PACK * HALF], F32, name="late")
         wg = [late[:, HOLD : HOLD + HALF], keep.tile([P, HALF], F32, name="wg1")[:]]
-        xq = [mx_tiles("x%d" % h, [P, 2, HALF]) for h in range(2)]
-        xb00 = keep.tile([P, HALF * PACK], BF16, name="xb00", align_bytes=64)
-        xb1 = keep.tile([P, 2 * HALF * PACK], BF16, name="xb1", align_bytes=64)
-        xb = {(0, 0): xb00[:], (1, 0): late[:, 3 * HALF :].bitcast(BF16)}
-        for a in range(2):
-            xb[a, 1] = xb1[:, a * HALF * PACK : (a + 1) * HALF * PACK]
+        xq = {}
+        xb = {}
         w1q = {}
         wb = {}
         for cb in range(2):
@@ -74,11 +69,11 @@ def tile_list_neighbour_shape_contrast_kernel(
 
         def load_x(a, i):
             rows = xT[a * KP : (a + 1) * KP, :].rearrange("(p i) t -> p i t", i=PACK)
-            planes[a, i] = stream.tile([P, T], F32, name="plane", tag="big")
+            planes[a, i] = keep.tile([P, T], F32, name="plane", tag="plane%d%d" % (a, i), align_bytes=64)
             nc.sync.dma_start(planes[a, i][:], rows[:, i, :])
 
         def load_w1(cb, a):
-            w1_raw[cb, a] = stream.tile([P, PACK, KP], F32, name="w1_raw", tag="big")
+            w1_raw[cb, a] = keep.tile([P, PACK, KP], F32, name="w1_raw", tag="plane0%d" % (2 * cb + a), align_bytes=64)
             nc.sync.dma_start(
                 w1_raw[cb, a][:],
                 w1[a * KP : (a + 1) * KP, cb * KP : (cb + 1) * KP].rearrange("(p j) c -> p j c", j=PACK),
@@ -127,7 +122,7 @@ def tile_list_neighbour_shape_contrast_kernel(
 
         def gather(a, i, h):
             if (a, i, h) == (1, 0, 1):
-                g4[a, h] = late[:, : PACK * HALF].rearrange("p (t c) -> p t c", t=PACK)
+                g4[a, h] = late[:].rearrange("p (t c) -> p t c", t=PACK)
             elif i == 0:
                 g4[a, h] = wide.tile([P, PACK, HALF], F32, name="g4", tag="wide")[:]
             j0 = h * HALF
@@ -139,17 +134,18 @@ def tile_list_neighbour_shape_contrast_kernel(
             )
 
         def weave_x(eng, a, h):
-            dst = xb[a, h].rearrange("p (c i t) -> p c t i", i=RUN, t=PACK)
+            tag = "xb0%d" % h if a == 0 else "xb1"
+            xb[a, h] = keep.tile([P, HALF * PACK], BF16, name="xb", tag=tag, align_bytes=64)
+            dst = xb[a, h][:].rearrange("p (c i t) -> p c t i", i=RUN, t=PACK)
             src = g4[a, h].rearrange("p t (c i) -> p c t i", i=RUN)
             cast(eng, dst, src)
 
-        def quant_x(h, passes, src):
-            codes, scales = xq[h]
-            nc.vector.quantize_mx(
-                codes[:, passes, :].rearrange("p a c -> p (a c)").bitcast(FP8X4),
-                scales[:, passes, :].rearrange("p a c -> p (a c)"),
-                src,
-            )
+        def quant_x(a, h):
+            tag = "plane13" if (a, h) == (0, 1) else "xc%d%d" % (a, h)
+            codes = keep.tile([P, HALF], U32, name="xc", tag=tag, align_bytes=64)
+            scales = keep.tile([P, HALF], U8, name="xs%d%d" % (a, h), align_bytes=64)
+            xq[a, h] = (codes, scales)
+            nc.vector.quantize_mx(codes[:].bitcast(FP8X4), scales[:], xb[a, h][:])
 
         def weave_w1(eng, cb, a, tp):
             dst = wb[cb, tp][:, a, :, :, :].rearrange("p t m j -> p m j t")
@@ -171,13 +167,13 @@ def tile_list_neighbour_shape_contrast_kernel(
             if a == 0:
                 bbank[cb, h, t] = psum.tile([P, HALF], F32, name="bank", tag="bank")
             c0 = cb * KP + t * P
-            codes, scales = xq[h]
+            codes, scales = xq[a, h]
             nc.tensor.matmul_mx(
                 bbank[cb, h, t][:],
                 lhsT=w2c[:, a, 2 * c0 : 2 * (c0 + P)].bitcast(FP4X4),
                 lhsT_scale=w2s[:, a, c0 : c0 + P],
-                rhs=codes[:, a, :].bitcast(FP8X4),
-                rhs_scale=scales[:, a, :],
+                rhs=codes[:].bitcast(FP8X4),
+                rhs_scale=scales[:],
                 start=(a == 0),
                 stop=(a == 1),
             )
@@ -195,36 +191,38 @@ def tile_list_neighbour_shape_contrast_kernel(
             b_pass(cb, h, t, 1)
             relu_b(eng, cb, h, t)
 
-        def a_sub(cb, j0, w):
+        diff = {}
+
+        def a_sub(cb, j0, w, tag):
             per = HALF // w
             h, jl = divmod(j0, HALF)
-            xcodes, xscales = xq[h]
+            diff[cb, j0] = keep.tile([P, PACK, w], F32, name="diff", tag=tag, align_bytes=64)
             for u in range(PACK // per):
                 bank = psum.tile([P, per, w], F32, name="bank", tag="bank")
                 for v in range(per):
                     tp, tt = divmod(u * per + v, 2)
                     codes, scales = w1q[cb, tp]
                     for a in range(2):
+                        xcodes, xscales = xq[a, h]
                         nc.tensor.matmul_mx(
                             bank[:, v, :],
                             lhsT=codes[:, a, tt * P : (tt + 1) * P].bitcast(FP8X4),
                             lhsT_scale=scales[:, a, tt * P : (tt + 1) * P],
-                            rhs=xcodes[:, a, jl : jl + w].bitcast(FP8X4),
-                            rhs_scale=xscales[:, a, jl : jl + w],
+                            rhs=xcodes[:, jl : jl + w].bitcast(FP8X4),
+                            rhs_scale=xscales[:, jl : jl + w],
                             start=(a == 0),
                             stop=(a == 1),
                         )
-                part = rb[cb, h][:, u * per : (u + 1) * per, jl : jl + w]
-                nc.vector.tensor_tensor(part, bank[:], part, ALU.subtract)
+                ts = slice(u * per, (u + 1) * per)
+                nc.vector.tensor_tensor(diff[cb, j0][:, ts, :], bank[:], rb[cb, h][:, ts, jl : jl + w], ALU.subtract)
 
         hb = {}
 
         def abs_h(cb, j0, w):
-            h, jl = divmod(j0, HALF)
             hb[cb, j0] = ring.tile([P, w, PACK], BF16, name="hb", tag="hb", align_bytes=64)
             nc.scalar.activation(
                 hb[cb, j0][:].rearrange("p (c i) t -> p c t i", i=RUN),
-                rb[cb, h][:, :, jl : jl + w].rearrange("p t (c i) -> p c t i", i=RUN),
+                diff[cb, j0][:].rearrange("p t (c i) -> p c t i", i=RUN),
                 ACT.Abs,
             )
 
@@ -236,69 +234,80 @@ def tile_list_neighbour_shape_contrast_kernel(
                 hb[cb, j0][:].rearrange("p c t -> p (c t)"),
             )
 
-        def y_tile(eng, j0, w, c):
-            cols = slice(j0, j0 + w)
-            res = keep.tile([P, w], F32, name="res%d_%d" % (j0, c))
-            bank = psum.tile([P, w], F32, name="bank", tag="bank")
-            for cb in range(2):
-                codes, scales = hq[cb]
-                nc.tensor.matmul_mx(
-                    bank[:],
-                    lhsT=w3c[:, cb, c * P : (c + 1) * P].bitcast(FP8X4),
-                    lhsT_scale=w3s[:, cb, c * P : (c + 1) * P],
-                    rhs=codes[:, cols].bitcast(FP8X4),
-                    rhs_scale=scales[:, cols],
-                    start=(cb == 0),
-                    stop=(cb == 1),
-                )
+        ybank = {}
+        res = [keep.tile([P, S], F32, name="res%d" % c) for c in range(N // P)]
+
+        def y_pass(j0, w, c, cb):
+            if cb == 0:
+                ybank[j0, c] = psum.tile([P, w], F32, name="bank", tag="bank")
+            codes, scales = hq[cb]
+            nc.tensor.matmul_mx(
+                ybank[j0, c][:],
+                lhsT=w3c[:, cb, c * P : (c + 1) * P].bitcast(FP8X4),
+                lhsT_scale=w3s[:, cb, c * P : (c + 1) * P],
+                rhs=codes[:, j0 : j0 + w].bitcast(FP8X4),
+                rhs_scale=scales[:, j0 : j0 + w],
+                start=(cb == 0),
+                stop=(cb == 1),
+            )
+
+        def y_out(eng, j0, w, c):
+            dst = res[c][:, j0 : j0 + w]
             if eng is nc.scalar:
-                nc.scalar.activation(res[:], bank[:], ACT.Identity, bias=bias[:, c : c + 1])
+                nc.scalar.activation(dst, ybank[j0, c][:], ACT.Identity, bias=bias[:, c : c + 1])
             else:
-                nc.vector.tensor_scalar(res[:], bank[:], bias[:, c : c + 1], None, ALU.add)
-            nc.sync.dma_start(out[c * P : (c + 1) * P, cols], res[:])
+                nc.vector.tensor_scalar(dst, ybank[j0, c][:], bias[:, c : c + 1], None, ALU.add)
+
+        def store(j0, w, c):
+            nc.sync.dma_start(out[c * P : (c + 1) * P, j0 : j0 + w], res[c][:, j0 : j0 + w])
+
+        def y_tile(eng, j0, w, c):
+            y_pass(j0, w, c, 0)
+            y_pass(j0, w, c, 1)
+            y_out(eng, j0, w, c)
 
         V, A = nc.vector, nc.scalar
 
+        load_w2()
         load_scales(s2_raw, w2_scales)
         load_wg(0)
         load_x(0, 0)
         load_wg(1)
         load_x(0, 1)
-        load_w2()
         for a in range(2):
             for i in range(PACK):
                 if (a, i) > (0, 1):
                     load_x(a, i)
-        for cb in range(2):
-            for a in range(2):
-                load_w1(cb, a)
-        load_w3()
 
+        deal_w2_words()
         deal_w2_scales()
         for i in range(PACK):
             for h in range(2):
                 gather(0, i, h)
-            if i == 1:
-                deal_w2_words()
+        for cb in range(2):
+            for a in range(2):
+                load_w1(cb, a)
+        load_w3()
         weave_x(A, 0, 0)
         weave_x(A, 0, 1)
-        gather(1, 0, 0)
-        gather(1, 0, 1)
-        for i in range(1, PACK):
+        for i in range(2):
+            for h in range(2):
+                gather(1, i, h)
+        quant_x(0, 0)
+        for i in range(2, PACK):
             gather(1, i, 0)
-        quant_x(0, slice(0, 1), xb[0, 0])
         for cb in range(2):
             for t in range(PACK):
                 b_pass(cb, 0, t, 0)
         weave_x(A, 1, 0)
-        gather(1, 1, 1)
-        gather(1, 2, 1)
-        quant_x(0, slice(1, 2), xb[1, 0])
-        gather(1, 3, 1)
+        for i in reversed(range(2, PACK)):
+            gather(1, i, 1)
+        quant_x(0, 1)
+        quant_x(1, 0)
         weave_w1(A, 0, 0, 0)
         weave_w1(A, 0, 0, 1)
         weave_x(V, 1, 1)
-        quant_x(1, slice(0, 2), xb1[:])
+        quant_x(1, 1)
         for cb in range(2):
             for t in range(PACK):
                 b_pass(cb, 0, t, 1)
@@ -307,36 +316,52 @@ def tile_list_neighbour_shape_contrast_kernel(
             weave_w1(V, 0, 1, tp)
         for tp in range(2):
             quant_w1(0, tp)
-        for t in range(PACK):
-            b_tile(A, 0, 1, t)
+        last = S - P
+
+        def h_step(cb, j0, w, tag):
+            a_sub(cb, j0, w, tag)
+            abs_h(cb, j0, w)
+
+        def y_step(engines, j0, w):
+            for c in range(N // P):
+                y_tile(engines[c], j0, w, c)
+                store(j0, w, c)
+
         for tp in range(2):
             weave_w1(V, 1, 0, tp)
-        a_sub(0, 0, UNIT)
-        abs_h(0, 0, UNIT)
+        for t in range(PACK):
+            b_tile(A, 0, 1, t)
+        h_step(0, 0, UNIT, "plane02")
         for tp in range(2):
             weave_w1(V, 1, 1, tp)
-        for t in range(2):
-            b_tile(A, 1, 1, t)
-        a_sub(0, UNIT, UNIT)
-        abs_h(0, UNIT, UNIT)
         for tp in range(2):
             quant_w1(1, tp)
-        for t in range(2, PACK):
-            b_tile(A, 1, 1, t)
-        steps = [(0, 2 * UNIT, UNIT), (0, 3 * UNIT, UNIT), (1, 0, UNIT), (1, UNIT, UNIT), (1, 2 * UNIT, UNIT)]
-        steps = steps + [(1, 3 * UNIT, P), (1, 3 * UNIT + P, P)]
-        waiting = [(0, 0, UNIT), (0, UNIT, UNIT)]
-        for step in steps:
-            a_sub(*step)
-            abs_h(*step)
-            quant_h(*waiting[0])
-            waiting = waiting[1:] + [step]
-        for step in waiting[:1]:
-            quant_h(*step)
+        for t in range(PACK):
+            b_tile((A, A, A, A)[t], 1, 1, t)
+        h_step(0, UNIT, UNIT, "plane03")
+        quant_h(0, 0, UNIT)
+        h_step(1, 0, UNIT, "plane10")
+        quant_h(0, UNIT, UNIT)
+        h_step(1, UNIT, UNIT, "plane12")
+        quant_h(1, 0, UNIT)
+        h_step(0, HALF, UNIT, "plane00")
+        quant_h(1, UNIT, UNIT)
+        h_step(1, HALF, UNIT, "plane01")
+        quant_h(0, HALF, UNIT)
+        h_step(0, HALF + UNIT, UNIT, "plane02")
+        y_step((A, V, A), 0, HALF)
+        quant_h(1, HALF, UNIT)
+        h_step(1, last - P, P, "plane03")
+        h_step(1, last, P, "plane10")
+        quant_h(0, HALF + UNIT, UNIT)
+        y_step((V, V, V), HALF, UNIT)
+        quant_h(1, last - P, P)
         for c in range(N // P):
-            y_tile(A if c % 2 == 0 else V, 0, HALF, c)
+            y_tile((V, A, V)[c], last - P, P, c)
         for c in range(N // P):
-            y_tile(A if c % 2 == 0 else V, HALF, UNIT, c)
-        quant_h(*waiting[1])
+            y_pass(last, P, c, 0)
+        quant_h(1, last, P)
         for c in range(N // P):
-            y_tile(V if c % 2 == 0 else A, HALF + UNIT, UNIT, c)
+            y_pass(last, P, c, 1)
+            y_out((A, V, A)[c], last, P, c)
+            store(last - P, 2 * P, c)

@@ -21,7 +21,7 @@ PACK = 4
 KP = P * PACK
 HALF = 512
 UNIT = 256
-RUN = 4
+RUN = 2
 HOLD = 1024
 
 

@@ -120,24 +120,24 @@ def tile_list_neighbour_shape_contrast_kernel(
 
         g4 = {}
 
-        def gather(a, i, h):
+        def gather(a, i, h, lo=0, w=HALF):
             if (a, i, h) == (1, 0, 1):
                 g4[a, h] = late[:].rearrange("p (t c) -> p t c", t=PACK)
             elif i == 0:
                 g4[a, h] = wide.tile([P, PACK, HALF], F32, name="g4", tag="wide")[:]
-            j0 = h * HALF
+            j0 = h * HALF + lo
             nc.vector.tensor_tensor(
-                g4[a, h][:, i, :],
-                planes[a, i][:].indirect(offsets[:, j0 // 16 : (j0 + HALF) // 16]),
-                wg[h],
+                g4[a, h][:, i, lo : lo + w],
+                planes[a, i][:].indirect(offsets[:, j0 // 16 : (j0 + w) // 16]),
+                wg[h][:, lo : lo + w],
                 ALU.mult,
             )
 
-        def weave_x(eng, a, h):
-            tag = "xb0%d" % h if a == 0 else "xb1"
-            xb[a, h] = keep.tile([P, HALF * PACK], BF16, name="xb", tag=tag, align_bytes=64)
-            dst = xb[a, h][:].rearrange("p (c i t) -> p c t i", i=RUN, t=PACK)
-            src = g4[a, h].rearrange("p t (c i) -> p c t i", i=RUN)
+        def weave_x(eng, a, h, t0=0, nt=PACK, lo=0, w=HALF):
+            if (a, h) not in xb:
+                xb[a, h] = keep.tile([P, HALF, PACK], BF16, name="xb", tag="xb%d%d" % (a, h), align_bytes=64)
+            dst = xb[a, h][:, lo : lo + w, :].rearrange("p (c i) t -> p c t i", i=RUN)[:, :, t0 : t0 + nt, :]
+            src = g4[a, h][:, t0 : t0 + nt, lo : lo + w].rearrange("p t (c i) -> p c t i", i=RUN)
             cast(eng, dst, src)
 
         def quant_x(a, h):
@@ -145,7 +145,7 @@ def tile_list_neighbour_shape_contrast_kernel(
             codes = keep.tile([P, HALF], U32, name="xc", tag=tag, align_bytes=64)
             scales = keep.tile([P, HALF], U8, name="xs%d%d" % (a, h), align_bytes=64)
             xq[a, h] = (codes, scales)
-            nc.vector.quantize_mx(codes[:].bitcast(FP8X4), scales[:], xb[a, h][:])
+            nc.vector.quantize_mx(codes[:].bitcast(FP8X4), scales[:], xb[a, h][:].rearrange("p c t -> p (c t)"))
 
         def weave_w1(eng, cb, a, tp):
             dst = wb[cb, tp][:, a, :, :, :].rearrange("p t m j -> p m j t")
@@ -294,19 +294,22 @@ def tile_list_neighbour_shape_contrast_kernel(
             for h in range(2):
                 gather(1, i, h)
         quant_x(0, 0)
-        for i in range(2, PACK):
-            gather(1, i, 0)
+        for h in range(2):
+            weave_x(A, 1, h, 0, 2)
+        gather(1, 2, 0)
+        for lo in (0, UNIT):
+            gather(1, 3, 0, lo, UNIT)
+            weave_x(A, 1, 0, 2, 2, lo, UNIT)
         for cb in range(2):
             for t in range(PACK):
                 b_pass(cb, 0, t, 0)
-        weave_x(A, 1, 0)
-        for i in reversed(range(2, PACK)):
-            gather(1, i, 1)
-        quant_x(0, 1)
+        gather(1, 3, 1)
+        gather(1, 2, 1)
         quant_x(1, 0)
+        weave_x(V, 1, 1, 2, 2)
+        quant_x(0, 1)
         weave_w1(A, 0, 0, 0)
         weave_w1(A, 0, 0, 1)
-        weave_x(V, 1, 1)
         quant_x(1, 1)
         for cb in range(2):
             for t in range(PACK):
@@ -329,9 +332,11 @@ def tile_list_neighbour_shape_contrast_kernel(
 
         for tp in range(2):
             weave_w1(V, 1, 0, tp)
-        for t in range(PACK):
+        for t in range(2):
             b_tile(A, 0, 1, t)
         h_step(0, 0, UNIT, "plane02")
+        for t in range(2, PACK):
+            b_tile(A, 0, 1, t)
         for tp in range(2):
             weave_w1(V, 1, 1, tp)
         for tp in range(2):

@@ -310,13 +310,13 @@ def tile_list_neighbour_shape_contrast_kernel(
         quant_x(0, 1)
         weave_w1(A, 0, 0, 0)
         weave_w1(A, 0, 0, 1)
+        weave_w1(A, 0, 1, 1)
         quant_x(1, 1)
         for cb in range(2):
             for t in range(PACK):
                 b_pass(cb, 0, t, 1)
                 relu_b(A, cb, 0, t)
-        for tp in range(2):
-            weave_w1(V, 0, 1, tp)
+        weave_w1(V, 0, 1, 0)
         for tp in range(2):
             quant_w1(0, tp)
         last = S - P

@@ -44,9 +44,10 @@ def tile_list_neighbour_shape_contrast_kernel(
             return codes, scales
 
         w2_raw = keep.tile([P, 2, 2 * H], U8, name="w2_raw", align_bytes=64)
-        s2_raw = keep.tile([P, 2, H], U8, name="s2_raw", align_bytes=64)
+        s2_raw = keep.tile([P, KP], U8, name="s2_raw", align_bytes=64)
+        s2_dealt = keep.tile([P, KP], U8, name="s2_dealt", align_bytes=64)
         w2c = keep.tile([P, 2, 2 * H], U8, name="w2c", align_bytes=64)
-        w2s = keep.tile([P, 2, H], U8, name="w2s", align_bytes=64)
+        w2s = keep.tile([P, 2, 2, KP], U8, name="w2s", align_bytes=64)
         w3c, w3s = mx_tiles("w3", [P, 2, N])
         bias = keep.tile([P, N // P], F32, name="bias")
         late = keep.tile([P, PACK * HALF], F32, name="late")
@@ -61,7 +62,8 @@ def tile_list_neighbour_shape_contrast_kernel(
                 wb[cb, tp] = keep.tile([P, 2, 2, P, PACK], BF16, name="wb%d%d" % (cb, tp), align_bytes=64)
         hq = [mx_tiles("h%d" % cb, [P, S]) for cb in range(2)]
 
-        nc.gpsimd.memset(s2_raw[:].bitcast(I32), 0)
+        nc.gpsimd.memset(s2_raw[P // 2 : P, :].bitcast(I32), 0)
+        nc.gpsimd.memset(w2s[:].rearrange("p b a c -> p (b a c)").bitcast(I32), 0)
         nc.gpsimd.memset(w3s[:].bitcast(I32), 0)
 
         planes = {}
@@ -89,6 +91,19 @@ def tile_list_neighbour_shape_contrast_kernel(
                     src[:, 4 * q : 4 * q + 4, :].rearrange("a q c -> q a c").bitcast(I32),
                 )
 
+        def load_s2():
+            nc.sync.dma_start(
+                s2_raw[0 : P // 2, :].bitcast(I32),
+                w2_scales.rearrange("a r (b c) -> (r b) a c", b=2).bitcast(I32),
+            )
+
+        def place_s2():
+            for q in range(4):
+                nc.sync.dma_start(
+                    w2s[32 * q : 32 * q + 4, :, :, :].rearrange("p b a c -> p (b a c)").bitcast(I32),
+                    s2_dealt[16 * q : 16 * q + 16, :].bitcast(I32),
+                )
+
         def load_w2():
             nc.sync.dma_start(w2_raw[:].bitcast(I32), w2_words.rearrange("a p c -> p a c").bitcast(I32))
 
@@ -106,8 +121,8 @@ def tile_list_neighbour_shape_contrast_kernel(
 
         def deal_w2_scales():
             nc.vector.tensor_copy(
-                w2s[:].rearrange("p a (b t m) -> p (a b) t m", b=2, t=PACK),
-                s2_raw[:].rearrange("p a (b m t) -> p (a b) t m", b=2, t=PACK),
+                s2_dealt[:].rearrange("p (t m) -> p t m", t=PACK),
+                s2_raw[:].rearrange("p (m t) -> p t m", t=PACK),
             )
 
         def cast(eng, dst, src):
@@ -171,7 +186,7 @@ def tile_list_neighbour_shape_contrast_kernel(
             nc.tensor.matmul_mx(
                 bbank[cb, h, t][:],
                 lhsT=w2c[:, a, 2 * c0 : 2 * (c0 + P)].bitcast(FP4X4),
-                lhsT_scale=w2s[:, a, c0 : c0 + P],
+                lhsT_scale=w2s[:, cb, a, t * P : (t + 1) * P],
                 rhs=codes[:].bitcast(FP8X4),
                 rhs_scale=scales[:],
                 start=(a == 0),
@@ -268,8 +283,8 @@ def tile_list_neighbour_shape_contrast_kernel(
 
         V, A = nc.vector, nc.scalar
 
+        load_s2()
         load_w2()
-        load_scales(s2_raw, w2_scales)
         load_wg(0)
         load_x(0, 0)
         load_wg(1)
@@ -279,8 +294,9 @@ def tile_list_neighbour_shape_contrast_kernel(
                 if (a, i) > (0, 1):
                     load_x(a, i)
 
-        deal_w2_words()
         deal_w2_scales()
+        deal_w2_words()
+        place_s2()
         for i in range(PACK):
             for h in range(2):
                 gather(0, i, h)

@@ -22,7 +22,7 @@ KP = P * PACK
 HALF = 512
 UNIT = 256
 RUN = 2
-HOLD = 1024
+RING = 4
 
 
 def tile_list_neighbour_shape_contrast_kernel(
@@ -31,27 +31,29 @@ def tile_list_neighbour_shape_contrast_kernel(
     nc = tc.nc
     with ExitStack() as ctx:
         keep = ctx.enter_context(tc.tile_pool(name="keep", bufs=1))
-        wide = ctx.enter_context(tc.tile_pool(name="wide", bufs=5))
-        ring = ctx.enter_context(tc.tile_pool(name="ring", bufs=6))
-        psum = ctx.enter_context(tc.psum_pool(name="psum", bufs=8))
+        wide = ctx.enter_context(tc.tile_pool(name="wide", bufs=4))
+        psum = ctx.enter_context(tc.psum_pool(name="psum", bufs=1))
 
         offsets = keep.tile([P, S // 16], U16, name="offsets")
         nc.sync.dma_start(offsets[:], offs)
+
+        def bank_tile(n, shape):
+            return psum.tile(shape, F32, name="bank", tag="bank%d" % n)
 
         def mx_tiles(name, shape):
             codes = keep.tile(shape, U32, name=name + "_codes", align_bytes=64)
             scales = keep.tile(shape, U8, name=name + "_scales", align_bytes=64)
             return codes, scales
 
-        w2_raw = keep.tile([P, 2, 2 * H], U8, name="w2_raw", align_bytes=64)
+        w2_raw = [keep.tile([P, 2 * H], U8, name="w2_raw", tag="w2_raw%d" % a, align_bytes=64) for a in range(2)]
         s2_raw = keep.tile([P, KP], U8, name="s2_raw", align_bytes=64)
         s2_dealt = keep.tile([P, KP], U8, name="s2_dealt", align_bytes=64)
-        w2c = keep.tile([P, 2, 2 * H], U8, name="w2c", align_bytes=64)
+        w2c = [keep.tile([P, 2 * H], U8, name="w2c%d" % a, align_bytes=64) for a in range(2)]
         w2s = keep.tile([P, 2, 2, KP], U8, name="w2s", align_bytes=64)
         w3c, w3s = mx_tiles("w3", [P, 2, N])
         bias = keep.tile([P, N // P], F32, name="bias")
-        late = keep.tile([P, PACK * HALF], F32, name="late")
-        wg = [late[:, HOLD : HOLD + HALF], keep.tile([P, HALF], F32, name="wg1")[:]]
+        late = keep.tile([P, 3 * HALF + S], F32, name="late", align_bytes=64)
+        wg = late[:, 3 * HALF : 3 * HALF + S]
         xq = {}
         xb = {}
         w1q = {}
@@ -60,11 +62,12 @@ def tile_list_neighbour_shape_contrast_kernel(
             for tp in range(2):
                 w1q[cb, tp] = mx_tiles("w1_%d%d" % (cb, tp), [P, 2, 2 * P])
                 wb[cb, tp] = keep.tile([P, 2, 2, P, PACK], BF16, name="wb%d%d" % (cb, tp), align_bytes=64)
-        hq = [mx_tiles("h%d" % cb, [P, S]) for cb in range(2)]
+        hq = [mx_tiles("h%d" % g, [P, 2, UNIT]) for g in range(S // UNIT)]
+        hb = [keep.tile([P, 2, UNIT * PACK], BF16, name="hb%d" % g, align_bytes=64) for g in range(S // UNIT)]
 
-        nc.gpsimd.memset(s2_raw[P // 2 : P, :].bitcast(I32), 0)
-        nc.gpsimd.memset(w2s[:].rearrange("p b a c -> p (b a c)").bitcast(I32), 0)
-        nc.gpsimd.memset(w3s[:].bitcast(I32), 0)
+        nc.vector.memset(s2_raw[P // 2 : P, :].bitcast(I32), 0)
+        nc.vector.memset(w2s[:].rearrange("p b a c -> p (b a c)").bitcast(I32), 0)
+        nc.vector.memset(w3s[:].bitcast(I32), 0)
 
         planes = {}
         w1_raw = {}
@@ -82,7 +85,7 @@ def tile_list_neighbour_shape_contrast_kernel(
             )
 
         def load_wg(h):
-            nc.sync.dma_start(wg[h], wgt[:, h * HALF : (h + 1) * HALF])
+            nc.sync.dma_start(wg[:, h * HALF : (h + 1) * HALF], wgt[:, h * HALF : (h + 1) * HALF])
 
         def load_scales(dst, src):
             for q in range(4):
@@ -104,8 +107,8 @@ def tile_list_neighbour_shape_contrast_kernel(
                     s2_dealt[16 * q : 16 * q + 16, :].bitcast(I32),
                 )
 
-        def load_w2():
-            nc.sync.dma_start(w2_raw[:].bitcast(I32), w2_words.rearrange("a p c -> p a c").bitcast(I32))
+        def load_w2(a):
+            nc.sync.dma_start(w2_raw[a][:].bitcast(I32), w2_words[a].bitcast(I32))
 
         def load_w3():
             nc.sync.dma_start(w3c[:].bitcast(I32), w3_words.rearrange("a p c i -> p a (c i)").bitcast(I32))
@@ -113,10 +116,10 @@ def tile_list_neighbour_shape_contrast_kernel(
             with nc.allow_non_contiguous_dma(reason="one bias value to a partition"):
                 nc.sync.dma_start(bias[:], b3.rearrange("(c p) -> p c", p=P))
 
-        def deal_w2_words():
-            nc.vector.tensor_copy(
-                w2c[:].bitcast(U16).rearrange("p a (b t m) -> p (a b) t m", b=2, t=PACK),
-                w2_raw[:].bitcast(U16).rearrange("p a (b m t) -> p (a b) t m", b=2, t=PACK),
+        def deal_w2_words(a, cb0=0, cb1=2):
+            nc.scalar.copy(
+                w2c[a][:].bitcast(U16).rearrange("p (b t m) -> p b t m", b=2, t=PACK)[:, cb0:cb1],
+                w2_raw[a][:].bitcast(U16).rearrange("p (b m t) -> p b t m", b=2, t=PACK)[:, cb0:cb1],
             )
 
         def deal_w2_scales():
@@ -128,39 +131,44 @@ def tile_list_neighbour_shape_contrast_kernel(
         def cast(eng, dst, src):
             if eng is nc.scalar:
                 nc.scalar.copy(dst, src)
-            elif eng is nc.gpsimd:
-                nc.gpsimd.tensor_scalar(dst, src, 1.0, 0.0, ALU.mult, ALU.add)
             else:
                 nc.vector.tensor_copy(dst, src)
 
-        g4 = {}
+        picked = {
+            (1, 0, 1): late[:, 0 : 2 * HALF].rearrange("p (t c) -> p t c", t=2),
+            (1, 1, 1): late[:, HALF + UNIT : 3 * HALF + UNIT].rearrange("p (t c) -> p t c", t=2),
+        }
+        both = {}
+        for a, u in ((0, 0), (0, 1), (1, 0)):
+            both[a, u] = wide.tile([P, 2 * S], F32, name="both", tag="wide")[:].rearrange("p (t c) -> p t c", t=2)
+            for h in range(2):
+                picked[a, h, u] = both[a, u][:, :, h * HALF : (h + 1) * HALF]
+        for a in range(2):
+            for h in range(2):
+                xb[a, h] = keep.tile([P, HALF * PACK], BF16, name="xb%d%d" % (a, h), align_bytes=64)[:]
 
-        def gather(a, i, h, lo=0, w=HALF):
-            if (a, i, h) == (1, 0, 1):
-                g4[a, h] = late[:].rearrange("p (t c) -> p t c", t=PACK)
-            elif i == 0:
-                g4[a, h] = wide.tile([P, PACK, HALF], F32, name="g4", tag="wide")[:]
-            j0 = h * HALF + lo
+        def gather(a, i, j0, w):
+            u, e = divmod(i, 2)
+            h, lo = divmod(j0, HALF)
+            dst = both[a, u][:, e, :] if w == S else picked[a, h, u][:, e, lo : lo + w]
             nc.vector.tensor_tensor(
-                g4[a, h][:, i, lo : lo + w],
+                dst,
                 planes[a, i][:].indirect(offsets[:, j0 // 16 : (j0 + w) // 16]),
-                wg[h][:, lo : lo + w],
+                wg[:, j0 : j0 + w],
                 ALU.mult,
             )
 
-        def weave_x(eng, a, h, t0=0, nt=PACK, lo=0, w=HALF):
-            if (a, h) not in xb:
-                xb[a, h] = keep.tile([P, HALF, PACK], BF16, name="xb", tag="xb%d%d" % (a, h), align_bytes=64)
-            dst = xb[a, h][:, lo : lo + w, :].rearrange("p (c i) t -> p c t i", i=RUN)[:, :, t0 : t0 + nt, :]
-            src = g4[a, h][:, t0 : t0 + nt, lo : lo + w].rearrange("p t (c i) -> p c t i", i=RUN)
-            cast(eng, dst, src)
+        def weave_x(eng, a, h, u, lo=0, w=HALF):
+            dst = xb[a, h][:, PACK * lo : PACK * (lo + w)].rearrange("p (c i t) -> p c t i", i=RUN, t=PACK)
+            src = picked[a, h, u][:, :, lo : lo + w].rearrange("p t (c i) -> p c t i", i=RUN)
+            cast(eng, dst[:, :, 2 * u : 2 * u + 2, :], src)
 
         def quant_x(a, h):
-            tag = "plane13" if (a, h) == (0, 1) else "xc%d%d" % (a, h)
+            tag = {(0, 0): "w2_raw0", (0, 1): "w2_raw1"}.get((a, h), "xc%d%d" % (a, h))
             codes = keep.tile([P, HALF], U32, name="xc", tag=tag, align_bytes=64)
             scales = keep.tile([P, HALF], U8, name="xs%d%d" % (a, h), align_bytes=64)
             xq[a, h] = (codes, scales)
-            nc.vector.quantize_mx(codes[:].bitcast(FP8X4), scales[:], xb[a, h][:].rearrange("p c t -> p (c t)"))
+            nc.vector.quantize_mx(codes[:].bitcast(FP8X4), scales[:], xb[a, h])
 
         def weave_w1(eng, cb, a, tp):
             dst = wb[cb, tp][:, a, :, :, :].rearrange("p t m j -> p m j t")
@@ -180,12 +188,12 @@ def tile_list_neighbour_shape_contrast_kernel(
 
         def b_pass(cb, h, t, a):
             if a == 0:
-                bbank[cb, h, t] = psum.tile([P, HALF], F32, name="bank", tag="bank")
+                bbank[cb, h, t] = bank_tile(cb * PACK + t, [P, HALF])
             c0 = cb * KP + t * P
             codes, scales = xq[a, h]
             nc.tensor.matmul_mx(
                 bbank[cb, h, t][:],
-                lhsT=w2c[:, a, 2 * c0 : 2 * (c0 + P)].bitcast(FP4X4),
+                lhsT=w2c[a][:, 2 * c0 : 2 * (c0 + P)].bitcast(FP4X4),
                 lhsT_scale=w2s[:, cb, a, t * P : (t + 1) * P],
                 rhs=codes[:].bitcast(FP8X4),
                 rhs_scale=scales[:],
@@ -194,7 +202,7 @@ def tile_list_neighbour_shape_contrast_kernel(
             )
 
         def relu_b(eng, cb, h, t):
-            if (cb, h) not in rb:
+            if t == 0:
                 rb[cb, h] = wide.tile([P, PACK, HALF], F32, name="rb", tag="wide")
             if eng is nc.scalar:
                 nc.scalar.activation(rb[cb, h][:, t, :], bbank[cb, h, t][:], ACT.Relu)
@@ -208,12 +216,19 @@ def tile_list_neighbour_shape_contrast_kernel(
 
         diff = {}
 
-        def a_sub(cb, j0, w, tag):
+        def diff_tiles(tag, w, steps):
+            room = keep.tile([P, len(steps), PACK, w], F32, name="diff", tag=tag, align_bytes=64)
+            for n, step in enumerate(steps):
+                diff[step] = room[:, n, :, :]
+
+        abanks = []
+
+        def a_sub(cb, j0, w):
             per = HALF // w
             h, jl = divmod(j0, HALF)
-            diff[cb, j0] = keep.tile([P, PACK, w], F32, name="diff", tag=tag, align_bytes=64)
             for u in range(PACK // per):
-                bank = psum.tile([P, per, w], F32, name="bank", tag="bank")
+                bank = bank_tile(len(abanks) % RING, [P, per, w])
+                abanks.append(bank)
                 for v in range(per):
                     tp, tt = divmod(u * per + v, 2)
                     codes, scales = w1q[cb, tp]
@@ -231,37 +246,38 @@ def tile_list_neighbour_shape_contrast_kernel(
                 ts = slice(u * per, (u + 1) * per)
                 nc.vector.tensor_tensor(diff[cb, j0][:, ts, :], bank[:], rb[cb, h][:, ts, jl : jl + w], ALU.subtract)
 
-        hb = {}
-
         def abs_h(cb, j0, w):
-            hb[cb, j0] = ring.tile([P, w, PACK], BF16, name="hb", tag="hb", align_bytes=64)
+            g, lo = divmod(j0, UNIT)
             nc.scalar.activation(
-                hb[cb, j0][:].rearrange("p (c i) t -> p c t i", i=RUN),
-                diff[cb, j0][:].rearrange("p t (c i) -> p c t i", i=RUN),
+                hb[g][:, cb, PACK * lo : PACK * (lo + w)].rearrange("p (c i t) -> p c t i", i=RUN, t=PACK),
+                diff[cb, j0].rearrange("p t (c i) -> p c t i", i=RUN),
                 ACT.Abs,
             )
 
-        def quant_h(cb, j0, w):
-            codes, scales = hq[cb]
+        def quant_h(g, c0=0, c1=2 * UNIT):
+            codes, scales = hq[g]
             nc.vector.quantize_mx(
-                codes[:, j0 : j0 + w].bitcast(FP8X4),
-                scales[:, j0 : j0 + w],
-                hb[cb, j0][:].rearrange("p c t -> p (c t)"),
+                codes[:].rearrange("p b c -> p (b c)")[:, c0:c1].bitcast(FP8X4),
+                scales[:].rearrange("p b c -> p (b c)")[:, c0:c1],
+                hb[g][:].rearrange("p b c -> p (b c)")[:, PACK * c0 : PACK * c1],
             )
 
         ybank = {}
+        last = S - P
         res = [keep.tile([P, S], F32, name="res%d" % c) for c in range(N // P)]
 
         def y_pass(j0, w, c, cb):
             if cb == 0:
-                ybank[j0, c] = psum.tile([P, w], F32, name="bank", tag="bank")
-            codes, scales = hq[cb]
+                n = len(ybank)
+                ybank[j0, c] = bank_tile(RING + n % RING if j0 < last else c, [P, w])
+            g, lo = divmod(j0, UNIT)
+            codes, scales = hq[g]
             nc.tensor.matmul_mx(
                 ybank[j0, c][:],
                 lhsT=w3c[:, cb, c * P : (c + 1) * P].bitcast(FP8X4),
                 lhsT_scale=w3s[:, cb, c * P : (c + 1) * P],
-                rhs=codes[:, j0 : j0 + w].bitcast(FP8X4),
-                rhs_scale=scales[:, j0 : j0 + w],
+                rhs=codes[:, cb, lo : lo + w].bitcast(FP8X4),
+                rhs_scale=scales[:, cb, lo : lo + w],
                 start=(cb == 0),
                 stop=(cb == 1),
             )
@@ -283,62 +299,8 @@ def tile_list_neighbour_shape_contrast_kernel(
 
         V, A = nc.vector, nc.scalar
 
-        load_s2()
-        load_w2()
-        load_wg(0)
-        load_x(0, 0)
-        load_wg(1)
-        load_x(0, 1)
-        for a in range(2):
-            for i in range(PACK):
-                if (a, i) > (0, 1):
-                    load_x(a, i)
-
-        deal_w2_scales()
-        deal_w2_words()
-        place_s2()
-        for i in range(PACK):
-            for h in range(2):
-                gather(0, i, h)
-        for cb in range(2):
-            for a in range(2):
-                load_w1(cb, a)
-        load_w3()
-        weave_x(A, 0, 0)
-        weave_x(A, 0, 1)
-        for i in range(2):
-            for h in range(2):
-                gather(1, i, h)
-        quant_x(0, 0)
-        for h in range(2):
-            weave_x(A, 1, h, 0, 2)
-        gather(1, 2, 0)
-        for lo in (0, UNIT):
-            gather(1, 3, 0, lo, UNIT)
-            weave_x(A, 1, 0, 2, 2, lo, UNIT)
-        for cb in range(2):
-            for t in range(PACK):
-                b_pass(cb, 0, t, 0)
-        gather(1, 3, 1)
-        gather(1, 2, 1)
-        quant_x(1, 0)
-        weave_x(V, 1, 1, 2, 2)
-        quant_x(0, 1)
-        weave_w1(A, 0, 0, 0)
-        weave_w1(A, 0, 0, 1)
-        weave_w1(A, 0, 1, 1)
-        quant_x(1, 1)
-        for cb in range(2):
-            for t in range(PACK):
-                b_pass(cb, 0, t, 1)
-                relu_b(A, cb, 0, t)
-        weave_w1(V, 0, 1, 0)
-        for tp in range(2):
-            quant_w1(0, tp)
-        last = S - P
-
-        def h_step(cb, j0, w, tag):
-            a_sub(cb, j0, w, tag)
+        def h_step(cb, j0, w):
+            a_sub(cb, j0, w)
             abs_h(cb, j0, w)
 
         def y_step(engines, j0, w):
@@ -346,43 +308,115 @@ def tile_list_neighbour_shape_contrast_kernel(
                 y_tile(engines[c], j0, w, c)
                 store(j0, w, c)
 
+        load_s2()
+        load_wg(0)
+        load_x(0, 0)
+        load_wg(1)
+        for i in range(1, PACK):
+            load_x(0, i)
+        deal_w2_scales()
+        for i in range(2):
+            load_x(1, i)
+        load_w2(0)
+        place_s2()
+        for i in range(2, PACK):
+            load_x(1, i)
+        load_w2(1)
+
+        for i in range(2):
+            gather(0, i, 0, S)
+        for h in range(2):
+            weave_x(A, 0, h, 0)
+        gather(0, 2, 0, S)
+        for h in range(2):
+            gather(0, 3, h * HALF, HALF)
+            weave_x(A, 0, h, 1)
+        for cb in range(2):
+            for a in range(2):
+                load_w1(cb, a)
+        load_w3()
+        deal_w2_words(0)
+        gather(1, 0, 0, S)
+        for h in range(2):
+            gather(1, 1, h * HALF, HALF)
+        quant_x(0, 0)
+        for h in range(2):
+            weave_x(A, 1, h, 0)
+        for cb in range(2):
+            for t in range(PACK):
+                b_pass(cb, 0, t, 0)
+        gather(1, 2, 0, HALF)
+        for lo in (0, UNIT):
+            gather(1, 3, lo, UNIT)
+            weave_x(A, 1, 0, 1, lo, UNIT)
+        for cb in range(2):
+            deal_w2_words(1, cb, cb + 1)
+        gather(1, 3, HALF, HALF)
+        quant_x(1, 0)
+        for cb in range(2):
+            for t in range(PACK):
+                b_pass(cb, 0, t, 1)
+                relu_b(A, cb, 0, t)
+        gather(1, 2, HALF, HALF)
+        quant_x(0, 1)
+        weave_w1(V, 0, 0, 0)
+        weave_x(V, 1, 1, 1)
+        weave_w1(V, 0, 0, 1)
+        quant_x(1, 1)
+        weave_w1(A, 1, 0, 1)
+        for cb in range(2):
+            for t in range(PACK):
+                b_tile(A, cb, 1, t)
         for tp in range(2):
-            weave_w1(V, 1, 0, tp)
-        for t in range(2):
-            b_tile(A, 0, 1, t)
-        h_step(0, 0, UNIT, "plane02")
-        for t in range(2, PACK):
-            b_tile(A, 0, 1, t)
+            weave_w1(V, 0, 1, tp)
+        for tp in range(2):
+            quant_w1(0, tp)
+        weave_w1(V, 1, 0, 0)
         for tp in range(2):
             weave_w1(V, 1, 1, tp)
+        diff_tiles("plane03", UNIT, [(0, 0), (0, UNIT)])
+        diff_tiles("plane10", UNIT, [(1, 0), (1, UNIT)])
+        diff_tiles("plane11", UNIT, [(0, HALF), (1, HALF)])
+        diff_tiles("plane12", UNIT, [(0, HALF + UNIT)])
+        diff_tiles("plane13", P, [(1, last - P), (1, last)])
         for tp in range(2):
             quant_w1(1, tp)
-        for t in range(PACK):
-            b_tile((A, A, A, A)[t], 1, 1, t)
-        h_step(0, UNIT, UNIT, "plane03")
-        quant_h(0, 0, UNIT)
-        h_step(1, 0, UNIT, "plane10")
-        quant_h(0, UNIT, UNIT)
-        h_step(1, UNIT, UNIT, "plane12")
-        quant_h(1, 0, UNIT)
-        h_step(0, HALF, UNIT, "plane00")
-        quant_h(1, UNIT, UNIT)
-        h_step(1, HALF, UNIT, "plane01")
-        quant_h(0, HALF, UNIT)
-        h_step(0, HALF + UNIT, UNIT, "plane02")
-        y_step((A, V, A), 0, HALF)
-        quant_h(1, HALF, UNIT)
-        h_step(1, last - P, P, "plane03")
-        h_step(1, last, P, "plane10")
-        quant_h(0, HALF + UNIT, UNIT)
-        y_step((V, V, V), HALF, UNIT)
-        quant_h(1, last - P, P)
+        h_step(0, 0, UNIT)
+        h_step(1, 0, UNIT)
+        h_step(0, UNIT, UNIT)
+        quant_h(0)
+        a_sub(1, UNIT, UNIT)
+        y_step((A, A, A), 0, UNIT)
+        abs_h(1, UNIT, UNIT)
+        h_step(0, HALF, UNIT)
+        quant_h(1)
+        a_sub(1, HALF, UNIT)
+        y_step((A, A, A), UNIT, UNIT)
+        abs_h(1, HALF, UNIT)
+        h_step(0, HALF + UNIT, UNIT)
+        h_step(1, last - P, P)
+        h_step(1, last, P)
+        quant_h(2)
         for c in range(N // P):
-            y_tile((V, A, V)[c], last - P, P, c)
+            y_pass(HALF, UNIT, c, 0)
+            y_pass(HALF, UNIT, c, 1)
+        quant_h(3, 0, UNIT + P)
+        y_out(V, HALF, UNIT, 0)
+        store(HALF, UNIT, 0)
+        y_pass(last - P, P, 0, 0)
+        y_pass(last - P, P, 0, 1)
+        quant_h(3, UNIT + P, 2 * UNIT)
+        for c in range(1, N // P):
+            y_out((A, V, A)[c], HALF, UNIT, c)
+            store(HALF, UNIT, c)
+        for c in range(1, N // P):
+            y_pass(last - P, P, c, 0)
+            y_pass(last - P, P, c, 1)
         for c in range(N // P):
             y_pass(last, P, c, 0)
-        quant_h(1, last, P)
+        for c in range(N // P):
+            y_out((A, A, V)[c], last - P, P, c)
         for c in range(N // P):
             y_pass(last, P, c, 1)
-            y_out((A, V, A)[c], last, P, c)
+            y_out((V, A, V)[c], last, P, c)
             store(last - P, 2 * P, c)

@@ -23,6 +23,8 @@ HALF = 512
 UNIT = 256
 RUN = 2
 RING = 4
+GROUP = 16
+SQ = 32
 
 
 def tile_list_neighbour_shape_contrast_kernel(
@@ -65,9 +67,9 @@ def tile_list_neighbour_shape_contrast_kernel(
         hq = [mx_tiles("h%d" % g, [P, 2, UNIT]) for g in range(S // UNIT)]
         hb = [keep.tile([P, 2, UNIT * PACK], BF16, name="hb%d" % g, align_bytes=64) for g in range(S // UNIT)]
 
-        nc.vector.memset(s2_raw[P // 2 : P, :].bitcast(I32), 0)
-        nc.vector.memset(w2s[:].rearrange("p b a c -> p (b a c)").bitcast(I32), 0)
-        nc.vector.memset(w3s[:].bitcast(I32), 0)
+        nc.gpsimd.memset(s2_raw[P // 2 : P, :].bitcast(I32), 0)
+        nc.gpsimd.memset(w2s[:].rearrange("p b a c -> p (b a c)").bitcast(I32), 0)
+        nc.gpsimd.memset(w3s[:].bitcast(I32), 0)
 
         planes = {}
         w1_raw = {}
@@ -84,8 +86,28 @@ def tile_list_neighbour_shape_contrast_kernel(
                 w1[a * KP : (a + 1) * KP, cb * KP : (cb + 1) * KP].rearrange("(p j) c -> p j c", j=PACK),
             )
 
-        def load_wg(h):
-            nc.sync.dma_start(wg[:, h * HALF : (h + 1) * HALF], wgt[:, h * HALF : (h + 1) * HALF])
+        wrow = keep.tile([P, 2 * SQ], F32, name="wrow", align_bytes=64)
+        wcol = keep.tile([P, 2 * SQ], F32, name="wcol", align_bytes=64)
+        wrep = keep.tile([P, S], F32, name="wrep", align_bytes=64)
+
+        def load_wg():
+            rows = wgt.rearrange("(g i) (b r) -> g i b r", i=GROUP, b=GROUP)
+            nc.sync.dma_start(wrow[:], rows[:, 0, :, :])
+
+        def turn_wg():
+            for u in range(2):
+                nc.vector.transpose(wcol[:, u * SQ : (u + 1) * SQ], wrow[:, u * SQ : (u + 1) * SQ])
+
+        def repeat_wg(h):
+            b0, b1 = h * GROUP // 2, (h + 1) * GROUP // 2
+            src = wcol[:].rearrange("p (u e b) -> p b u e", u=2, e=2)[:, b0:b1]
+            nc.vector.tensor_copy(
+                wrep[:, h * HALF : (h + 1) * HALF].rearrange("p (b u e i) -> p b u e i", u=2, e=2, i=GROUP),
+                src.unsqueeze(4).to_broadcast([P, GROUP // 2, 2, 2, GROUP]),
+            )
+
+        def spread_wg(h):
+            nc.vector.transpose(wg[:, h * HALF : (h + 1) * HALF], wrep[:, h * HALF : (h + 1) * HALF])
 
         def load_scales(dst, src):
             for q in range(4):
@@ -100,12 +122,11 @@ def tile_list_neighbour_shape_contrast_kernel(
                 w2_scales.rearrange("a r (b c) -> (r b) a c", b=2).bitcast(I32),
             )
 
-        def place_s2():
-            for q in range(4):
-                nc.sync.dma_start(
-                    w2s[32 * q : 32 * q + 4, :, :, :].rearrange("p b a c -> p (b a c)").bitcast(I32),
-                    s2_dealt[16 * q : 16 * q + 16, :].bitcast(I32),
-                )
+        def place_s2(queue, q):
+            queue.dma_start(
+                w2s[32 * q : 32 * q + 4, :, :, :].rearrange("p b a c -> p (b a c)").bitcast(I32),
+                s2_dealt[16 * q : 16 * q + 16, :].bitcast(I32),
+            )
 
         def load_w2(a):
             nc.sync.dma_start(w2_raw[a][:].bitcast(I32), w2_words[a].bitcast(I32))
@@ -222,12 +243,14 @@ def tile_list_neighbour_shape_contrast_kernel(
                 diff[step] = room[:, n, :, :]
 
         abanks = []
+        last = S - P
 
         def a_sub(cb, j0, w):
             per = HALF // w
             h, jl = divmod(j0, HALF)
             for u in range(PACK // per):
-                bank = bank_tile(len(abanks) % RING, [P, per, w])
+                n = len(abanks)
+                bank = bank_tile(n if n < RING + 2 else (n - 2 + (j0 == last)) % RING, [P, per, w])
                 abanks.append(bank)
                 for v in range(per):
                     tp, tt = divmod(u * per + v, 2)
@@ -263,7 +286,6 @@ def tile_list_neighbour_shape_contrast_kernel(
             )
 
         ybank = {}
-        last = S - P
         res = [keep.tile([P, S], F32, name="res%d" % c) for c in range(N // P)]
 
         def y_pass(j0, w, c, cb):
@@ -308,19 +330,24 @@ def tile_list_neighbour_shape_contrast_kernel(
                 y_tile(engines[c], j0, w, c)
                 store(j0, w, c)
 
+        load_wg()
         load_s2()
-        load_wg(0)
-        load_x(0, 0)
-        load_wg(1)
-        for i in range(1, PACK):
+        for i in range(PACK):
             load_x(0, i)
+        turn_wg()
         deal_w2_scales()
+        for q in range(3):
+            place_s2(nc.scalar, q)
+        for h in range(2):
+            repeat_wg(h)
+        for h in range(2):
+            spread_wg(h)
         for i in range(2):
             load_x(1, i)
         load_w2(0)
-        place_s2()
         for i in range(2, PACK):
             load_x(1, i)
+        place_s2(nc.sync, 3)
         load_w2(1)
 
         for i in range(2):
@@ -359,19 +386,23 @@ def tile_list_neighbour_shape_contrast_kernel(
                 relu_b(A, cb, 0, t)
         gather(1, 2, HALF, HALF)
         quant_x(0, 1)
-        weave_w1(V, 0, 0, 0)
-        weave_x(V, 1, 1, 1)
-        weave_w1(V, 0, 0, 1)
-        quant_x(1, 1)
         weave_w1(A, 1, 0, 1)
         for cb in range(2):
             for t in range(PACK):
-                b_tile(A, cb, 1, t)
-        for tp in range(2):
-            weave_w1(V, 0, 1, tp)
-        for tp in range(2):
-            quant_w1(0, tp)
+                b_pass(cb, 1, t, 0)
+        weave_w1(V, 0, 0, 0)
+        weave_x(V, 1, 1, 1)
+        weave_w1(V, 0, 0, 1)
+        weave_w1(V, 0, 1, 0)
+        quant_x(1, 1)
+        for cb in range(2):
+            for t in range(PACK):
+                b_pass(cb, 1, t, 1)
+                relu_b(A, cb, 1, t)
+        quant_w1(0, 0)
+        weave_w1(V, 0, 1, 1)
         weave_w1(V, 1, 0, 0)
+        quant_w1(0, 1)
         for tp in range(2):
             weave_w1(V, 1, 1, tp)
         diff_tiles("plane03", UNIT, [(0, 0), (0, UNIT)])
@@ -381,41 +412,41 @@ def tile_list_neighbour_shape_contrast_kernel(
         diff_tiles("plane13", P, [(1, last - P), (1, last)])
         for tp in range(2):
             quant_w1(1, tp)
-        h_step(0, 0, UNIT)
-        h_step(1, 0, UNIT)
-        h_step(0, UNIT, UNIT)
-        quant_h(0)
-        a_sub(1, UNIT, UNIT)
-        y_step((A, A, A), 0, UNIT)
-        abs_h(1, UNIT, UNIT)
+        for cb in range(2):
+            for j0 in (0, UNIT):
+                h_step(cb, j0, UNIT)
         h_step(0, HALF, UNIT)
-        quant_h(1)
+        quant_h(0)
         a_sub(1, HALF, UNIT)
-        y_step((A, A, A), UNIT, UNIT)
+        y_step((A, A, A), 0, UNIT)
         abs_h(1, HALF, UNIT)
-        h_step(0, HALF + UNIT, UNIT)
+        quant_h(1)
+        a_sub(0, HALF + UNIT, UNIT)
+        y_step((A, A, A), UNIT, UNIT)
+        abs_h(0, HALF + UNIT, UNIT)
         h_step(1, last - P, P)
-        h_step(1, last, P)
         quant_h(2)
+        h_step(1, last, P)
         for c in range(N // P):
             y_pass(HALF, UNIT, c, 0)
             y_pass(HALF, UNIT, c, 1)
-        quant_h(3, 0, UNIT + P)
+        quant_h(3, 0, UNIT)
+        quant_h(3, UNIT, UNIT + P)
+        for c in range(N // P):
+            y_pass(last, P, c, 0)
         y_out(V, HALF, UNIT, 0)
         store(HALF, UNIT, 0)
         y_pass(last - P, P, 0, 0)
         y_pass(last - P, P, 0, 1)
         quant_h(3, UNIT + P, 2 * UNIT)
         for c in range(1, N // P):
-            y_out((A, V, A)[c], HALF, UNIT, c)
+            y_out(A, HALF, UNIT, c)
             store(HALF, UNIT, c)
         for c in range(1, N // P):
             y_pass(last - P, P, c, 0)
             y_pass(last - P, P, c, 1)
         for c in range(N // P):
-            y_pass(last, P, c, 0)
-        for c in range(N // P):
-            y_out((A, A, V)[c], last - P, P, c)
+            y_out((V, V, A)[c], last - P, P, c)
         for c in range(N // P):
             y_pass(last, P, c, 1)
             y_out((V, A, V)[c], last, P, c)

@@ -23,6 +23,8 @@ HALF = 512
 UNIT = 256
 RUN = 2
 RING = 4
+LATE_BANKS = (6, 7, 3, 1, 0, 2, 4, 5, 6)
+LAST_PIECES = ((0, 128), (128, 192), (320, 192))
 GROUP = 16
 SQ = 32
 
@@ -291,7 +293,7 @@ def tile_list_neighbour_shape_contrast_kernel(
         def y_pass(j0, w, c, cb):
             if cb == 0:
                 n = len(ybank)
-                ybank[j0, c] = bank_tile(RING + n % RING if j0 < last else c, [P, w])
+                ybank[j0, c] = bank_tile(LATE_BANKS[n - 6] if n >= 6 else RING + n % RING, [P, w])
             g, lo = divmod(j0, UNIT)
             codes, scales = hq[g]
             nc.tensor.matmul_mx(
@@ -373,9 +375,9 @@ def tile_list_neighbour_shape_contrast_kernel(
             for t in range(PACK):
                 b_pass(cb, 0, t, 0)
         gather(1, 2, 0, HALF)
-        for lo in (0, UNIT):
-            gather(1, 3, lo, UNIT)
-            weave_x(A, 1, 0, 1, lo, UNIT)
+        for lo, w in LAST_PIECES:
+            gather(1, 3, lo, w)
+            weave_x(A, 1, 0, 1, lo, w)
         for cb in range(2):
             deal_w2_words(1, cb, cb + 1)
         gather(1, 3, HALF, HALF)
@@ -422,31 +424,32 @@ def tile_list_neighbour_shape_contrast_kernel(
         abs_h(1, HALF, UNIT)
         quant_h(1)
         a_sub(0, HALF + UNIT, UNIT)
-        y_step((A, A, A), UNIT, UNIT)
+        for c in range(N // P):
+            y_pass(UNIT, UNIT, c, 0)
+            y_pass(UNIT, UNIT, c, 1)
+        y_out(A, UNIT, UNIT, 0)
+        store(UNIT, UNIT, 0)
         abs_h(0, HALF + UNIT, UNIT)
         h_step(1, last - P, P)
         quant_h(2)
         h_step(1, last, P)
+        for c in range(1, N // P):
+            y_out(V, UNIT, UNIT, c)
+            store(UNIT, UNIT, c)
+        quant_h(3, 0, UNIT + P)
         for c in range(N // P):
             y_pass(HALF, UNIT, c, 0)
             y_pass(HALF, UNIT, c, 1)
-        quant_h(3, 0, UNIT)
-        quant_h(3, UNIT, UNIT + P)
-        for c in range(N // P):
-            y_pass(last, P, c, 0)
         y_out(V, HALF, UNIT, 0)
         store(HALF, UNIT, 0)
-        y_pass(last - P, P, 0, 0)
-        y_pass(last - P, P, 0, 1)
         quant_h(3, UNIT + P, 2 * UNIT)
         for c in range(1, N // P):
             y_out(A, HALF, UNIT, c)
             store(HALF, UNIT, c)
-        for c in range(1, N // P):
-            y_pass(last - P, P, c, 0)
-            y_pass(last - P, P, c, 1)
         for c in range(N // P):
-            y_out((V, V, A)[c], last - P, P, c)
+            y_tile((A, V, A)[c], last - P, P, c)
+        for c in range(N // P):
+            y_pass(last, P, c, 0)
         for c in range(N // P):
             y_pass(last, P, c, 1)
             y_out((V, A, V)[c], last, P, c)

@@ -338,7 +338,7 @@ def tile_list_neighbour_shape_contrast_kernel(
             load_x(0, i)
         turn_wg()
         deal_w2_scales()
-        for q in range(3):
+        for q in (0, 2):
             place_s2(nc.scalar, q)
         for h in range(2):
             repeat_wg(h)
@@ -349,7 +349,8 @@ def tile_list_neighbour_shape_contrast_kernel(
         load_w2(0)
         for i in range(2, PACK):
             load_x(1, i)
-        place_s2(nc.sync, 3)
+        for q in (1, 3):
+            place_s2(nc.sync, q)
         load_w2(1)
 
         for i in range(2):
@@ -375,6 +376,7 @@ def tile_list_neighbour_shape_contrast_kernel(
             for t in range(PACK):
                 b_pass(cb, 0, t, 0)
         gather(1, 2, 0, HALF)
+        gather(1, 2, HALF + UNIT, UNIT)
         for lo, w in LAST_PIECES:
             gather(1, 3, lo, w)
             weave_x(A, 1, 0, 1, lo, w)
@@ -386,7 +388,7 @@ def tile_list_neighbour_shape_contrast_kernel(
             for t in range(PACK):
                 b_pass(cb, 0, t, 1)
                 relu_b(A, cb, 0, t)
-        gather(1, 2, HALF, HALF)
+        gather(1, 2, HALF, UNIT)
         quant_x(0, 1)
         weave_w1(A, 1, 0, 1)
         for cb in range(2):

@@ -23,6 +23,7 @@ HALF = 512
 UNIT = 256
 RUN = 2
 RING = 4
+A_BANKS = (4, 5, 2, 3, 6, 7, 0, 1, 2, 3, 0, 1, 2, 3, 0, 2)
 LATE_BANKS = (6, 7, 3, 1, 0, 2, 4, 5, 6)
 LAST_PIECES = ((0, 128), (128, 192), (320, 192))
 GROUP = 16
@@ -211,7 +212,8 @@ def tile_list_neighbour_shape_contrast_kernel(
 
         def b_pass(cb, h, t, a):
             if a == 0:
-                bbank[cb, h, t] = bank_tile(cb * PACK + t, [P, HALF])
+                n = cb * PACK + t
+                bbank[cb, h, t] = bank_tile(RING + (n + 2) % RING if (cb, h) == (1, 1) else n, [P, HALF])
             c0 = cb * KP + t * P
             codes, scales = xq[a, h]
             nc.tensor.matmul_mx(
@@ -252,7 +254,7 @@ def tile_list_neighbour_shape_contrast_kernel(
             h, jl = divmod(j0, HALF)
             for u in range(PACK // per):
                 n = len(abanks)
-                bank = bank_tile(n if n < RING + 2 else (n - 2 + (j0 == last)) % RING, [P, per, w])
+                bank = bank_tile(A_BANKS[n], [P, per, w])
                 abanks.append(bank)
                 for v in range(per):
                     tp, tt = divmod(u * per + v, 2)
@@ -391,34 +393,38 @@ def tile_list_neighbour_shape_contrast_kernel(
         gather(1, 2, HALF, UNIT)
         quant_x(0, 1)
         weave_w1(A, 1, 0, 1)
-        for cb in range(2):
-            for t in range(PACK):
-                b_pass(cb, 1, t, 0)
+        for t in range(PACK):
+            b_pass(0, 1, t, 0)
         weave_w1(V, 0, 0, 0)
         weave_x(V, 1, 1, 1)
         weave_w1(V, 0, 0, 1)
-        weave_w1(V, 0, 1, 0)
         quant_x(1, 1)
-        for cb in range(2):
-            for t in range(PACK):
-                b_pass(cb, 1, t, 1)
-                relu_b(A, cb, 1, t)
-        quant_w1(0, 0)
-        weave_w1(V, 0, 1, 1)
+        for t in range(PACK):
+            b_pass(0, 1, t, 1)
+            relu_b(A, 0, 1, t)
+        b_tile(A, 1, 1, 0)
+        for tp in range(2):
+            weave_w1(V, 0, 1, tp)
+        for tp in range(2):
+            quant_w1(0, tp)
         weave_w1(V, 1, 0, 0)
-        quant_w1(0, 1)
+        diff_tiles("plane01", UNIT, [(0, 0)])
+        a_sub(0, 0, UNIT)
+        for t in range(1, PACK):
+            b_tile(A, 1, 1, t)
+        abs_h(0, 0, UNIT)
         for tp in range(2):
             weave_w1(V, 1, 1, tp)
-        diff_tiles("plane03", UNIT, [(0, 0), (0, UNIT)])
+        diff_tiles("plane03", UNIT, [(0, UNIT)])
         diff_tiles("plane10", UNIT, [(1, 0), (1, UNIT)])
         diff_tiles("plane11", UNIT, [(0, HALF), (1, HALF)])
         diff_tiles("plane12", UNIT, [(0, HALF + UNIT)])
         diff_tiles("plane13", P, [(1, last - P), (1, last)])
         for tp in range(2):
             quant_w1(1, tp)
-        for cb in range(2):
-            for j0 in (0, UNIT):
-                h_step(cb, j0, UNIT)
+        h_step(0, UNIT, UNIT)
+        for j0 in (0, UNIT):
+            h_step(1, j0, UNIT)
         h_step(0, HALF, UNIT)
         quant_h(0)
         a_sub(1, HALF, UNIT)
@@ -426,13 +432,14 @@ def tile_list_neighbour_shape_contrast_kernel(
         abs_h(1, HALF, UNIT)
         quant_h(1)
         a_sub(0, HALF + UNIT, UNIT)
+        a_sub(1, last - P, P)
         for c in range(N // P):
             y_pass(UNIT, UNIT, c, 0)
             y_pass(UNIT, UNIT, c, 1)
         y_out(A, UNIT, UNIT, 0)
         store(UNIT, UNIT, 0)
         abs_h(0, HALF + UNIT, UNIT)
-        h_step(1, last - P, P)
+        abs_h(1, last - P, P)
         quant_h(2)
         h_step(1, last, P)
         for c in range(1, N // P):

@@ -40,7 +40,6 @@ def tile_list_neighbour_shape_contrast_kernel(
         psum = ctx.enter_context(tc.psum_pool(name="psum", bufs=1))
 
         offsets = keep.tile([P, S // 16], U16, name="offsets")
-        nc.sync.dma_start(offsets[:], offs)
 
         def bank_tile(n, shape):
             return psum.tile(shape, F32, name="bank", tag="bank%d" % n)
@@ -336,7 +335,9 @@ def tile_list_neighbour_shape_contrast_kernel(
 
         load_wg()
         load_s2()
-        for i in range(PACK):
+        load_x(0, 0)
+        nc.sync.dma_start(offsets[:], offs)
+        for i in range(1, PACK):
             load_x(0, i)
         turn_wg()
         deal_w2_scales()

@@ -51,7 +51,7 @@ def tile_list_neighbour_shape_contrast_kernel(
 
         w2_raw = [keep.tile([P, 2 * H], U8, name="w2_raw", tag="w2_raw%d" % a, align_bytes=64) for a in range(2)]
         s2_raw = keep.tile([P, KP], U8, name="s2_raw", align_bytes=64)
-        s2_dealt = keep.tile([P, KP], U8, name="s2_dealt", align_bytes=64)
+        dealt = {}
         w2c = [keep.tile([P, 2 * H], U8, name="w2c%d" % a, align_bytes=64) for a in range(2)]
         w2s = keep.tile([P, 2, 2, KP], U8, name="w2s", align_bytes=64)
         w3c, w3s = mx_tiles("w3", [P, 2, N])
@@ -89,7 +89,7 @@ def tile_list_neighbour_shape_contrast_kernel(
             )
 
         wrow = keep.tile([P, 2 * SQ], F32, name="wrow", align_bytes=64)
-        wcol = keep.tile([P, 2 * SQ], F32, name="wcol", align_bytes=64)
+        wcol = keep.tile([P, 2 * SQ], F32, name="wcol", tag="wcol", align_bytes=64)
         wrep = keep.tile([P, S], F32, name="wrep", align_bytes=64)
 
         def load_wg():
@@ -119,7 +119,7 @@ def tile_list_neighbour_shape_contrast_kernel(
                 )
 
         def load_s2():
-            nc.sync.dma_start(
+            nc.scalar.dma_start(
                 s2_raw[0 : P // 2, :].bitcast(I32),
                 w2_scales.rearrange("a r (b c) -> (r b) a c", b=2).bitcast(I32),
             )
@@ -127,7 +127,7 @@ def tile_list_neighbour_shape_contrast_kernel(
         def place_s2(queue, q):
             queue.dma_start(
                 w2s[32 * q : 32 * q + 4, :, :, :].rearrange("p b a c -> p (b a c)").bitcast(I32),
-                s2_dealt[16 * q : 16 * q + 16, :].bitcast(I32),
+                dealt[0][16 * q : 16 * q + 16, :].bitcast(I32),
             )
 
         def load_w2(a):
@@ -146,8 +146,9 @@ def tile_list_neighbour_shape_contrast_kernel(
             )
 
         def deal_w2_scales():
-            nc.vector.tensor_copy(
-                s2_dealt[:].rearrange("p (t m) -> p t m", t=PACK),
+            dealt[0] = keep.tile([P, KP], U8, name="s2_dealt", tag="wcol", align_bytes=64)
+            nc.gpsimd.tensor_copy(
+                dealt[0][:].rearrange("p (t m) -> p t m", t=PACK),
                 s2_raw[:].rearrange("p (m t) -> p t m", t=PACK),
             )
 
@@ -340,11 +341,11 @@ def tile_list_neighbour_shape_contrast_kernel(
         for i in range(1, PACK):
             load_x(0, i)
         turn_wg()
+        for h in range(2):
+            repeat_wg(h)
         deal_w2_scales()
         for q in (0, 2):
             place_s2(nc.scalar, q)
-        for h in range(2):
-            repeat_wg(h)
         for h in range(2):
             spread_wg(h)
         for i in range(2):

from contextlib import ExitStack

import concourse.mybir as mybir

K, T, S, H, N = 1024, 2048, 1024, 1024, 384
FLOPS = 2 * S * (2 * K * H + H * N)

F32 = mybir.dt.float32
BF16 = mybir.dt.bfloat16
I32 = mybir.dt.int32
U32 = mybir.dt.uint32
U16 = mybir.dt.uint16
U8 = mybir.dt.uint8
FP8X4 = mybir.dt.float8_e4m3fn_x4
FP4X4 = mybir.dt.float4_e2m1fn_x4
ALU = mybir.AluOpType
ACT = mybir.ActivationFunctionType

P = 128
PACK = 4
KP = P * PACK
HALF = 512
UNIT = 256
RUN = 2
RING = 4
A_BANKS = (4, 5, 2, 3, 6, 7, 0, 1, 2, 3, 0, 1, 2, 3, 0, 2)
LATE_BANKS = (6, 7, 3, 1, 0, 2, 4, 5, 6)
LAST_PIECES = ((0, 128), (128, 192), (320, 192))
GROUP = 16
SQ = 32


def tile_list_neighbour_shape_contrast_kernel(
    tc, xT, wgt, offs, w1, w2_words, w2_scales, w3_words, w3_scales, b3, out
):
    nc = tc.nc
    with ExitStack() as ctx:
        keep = ctx.enter_context(tc.tile_pool(name="keep", bufs=1))
        wide = ctx.enter_context(tc.tile_pool(name="wide", bufs=4))
        psum = ctx.enter_context(tc.psum_pool(name="psum", bufs=1))

        offsets = keep.tile([P, S // 16], U16, name="offsets")

        def bank_tile(n, shape):
            return psum.tile(shape, F32, name="bank", tag="bank%d" % n)

        def mx_tiles(name, shape):
            codes = keep.tile(shape, U32, name=name + "_codes", align_bytes=64)
            scales = keep.tile(shape, U8, name=name + "_scales", align_bytes=64)
            return codes, scales

        w2_raw = [keep.tile([P, 2 * H], U8, name="w2_raw", tag="w2_raw%d" % a, align_bytes=64) for a in range(2)]
        s2_raw = keep.tile([P, KP], U8, name="s2_raw", align_bytes=64)
        dealt = {}
        w2c = [keep.tile([P, 2 * H], U8, name="w2c%d" % a, align_bytes=64) for a in range(2)]
        w2s = keep.tile([P, 2, 2, KP], U8, name="w2s", align_bytes=64)
        w3c, w3s = mx_tiles("w3", [P, 2, N])
        bias = keep.tile([P, N // P], F32, name="bias")
        late = keep.tile([P, 3 * HALF + S], F32, name="late", align_bytes=64)
        wg = late[:, 3 * HALF : 3 * HALF + S]
        xq = {}
        xb = {}
        w1q = {}
        wb = {}
        for cb in range(2):
            for tp in range(2):
                w1q[cb, tp] = mx_tiles("w1_%d%d" % (cb, tp), [P, 2, 2 * P])
                wb[cb, tp] = keep.tile([P, 2, 2, P, PACK], BF16, name="wb%d%d" % (cb, tp), align_bytes=64)
        hq = [mx_tiles("h%d" % g, [P, 2, UNIT]) for g in range(S // UNIT)]
        hb = [keep.tile([P, 2, UNIT * PACK], BF16, name="hb%d" % g, align_bytes=64) for g in range(S // UNIT)]

        nc.gpsimd.memset(s2_raw[P // 2 : P, :].bitcast(I32), 0)
        nc.gpsimd.memset(w2s[:].rearrange("p b a c -> p (b a c)").bitcast(I32), 0)
        nc.gpsimd.memset(w3s[:].bitcast(I32), 0)

        planes = {}
        w1_raw = {}

        def load_x(a, i):
            rows = xT[a * KP : (a + 1) * KP, :].rearrange("(p i) t -> p i t", i=PACK)
            planes[a, i] = keep.tile([P, T], F32, name="plane", tag="plane%d%d" % (a, i), align_bytes=64)
            nc.sync.dma_start(planes[a, i][:], rows[:, i, :])

        def load_w1(cb, a):
            w1_raw[cb, a] = keep.tile([P, PACK, KP], F32, name="w1_raw", tag="plane0%d" % (2 * cb + a), align_bytes=64)
            nc.sync.dma_start(
                w1_raw[cb, a][:],
                w1[a * KP : (a + 1) * KP, cb * KP : (cb + 1) * KP].rearrange("(p j) c -> p j c", j=PACK),
            )

        wrow = keep.tile([P, 2 * SQ], F32, name="wrow", align_bytes=64)
        wcol = keep.tile([P, 2 * SQ], F32, name="wcol", tag="wcol", align_bytes=64)
        wrep = keep.tile([P, S], F32, name="wrep", align_bytes=64)

        def load_wg():
            rows = wgt.rearrange("(g i) (b r) -> g i b r", i=GROUP, b=GROUP)
            nc.sync.dma_start(wrow[:], rows[:, 0, :, :])

        def turn_wg():
            for u in range(2):
                nc.vector.transpose(wcol[:, u * SQ : (u + 1) * SQ], wrow[:, u * SQ : (u + 1) * SQ])

        def repeat_wg(h):
            b0, b1 = h * GROUP // 2, (h + 1) * GROUP // 2
            src = wcol[:].rearrange("p (u e b) -> p b u e", u=2, e=2)[:, b0:b1]
            nc.vector.tensor_copy(
                wrep[:, h * HALF : (h + 1) * HALF].rearrange("p (b u e i) -> p b u e i", u=2, e=2, i=GROUP),
                src.unsqueeze(4).to_broadcast([P, GROUP // 2, 2, 2, GROUP]),
            )

        def spread_wg(h):
            nc.vector.transpose(wg[:, h * HALF : (h + 1) * HALF], wrep[:, h * HALF : (h + 1) * HALF])

        def load_scales(dst, src):
            for q in range(4):
                nc.sync.dma_start(
                    dst[32 * q : 32 * q + 4, :, :].bitcast(I32),
                    src[:, 4 * q : 4 * q + 4, :].rearrange("a q c -> q a c").bitcast(I32),
                )

        def load_s2():
            nc.scalar.dma_start(
                s2_raw[0 : P // 2, :].bitcast(I32),
                w2_scales.rearrange("a r (b c) -> (r b) a c", b=2).bitcast(I32),
            )

        def place_s2(queue, q):
            queue.dma_start(
                w2s[32 * q : 32 * q + 4, :, :, :].rearrange("p b a c -> p (b a c)").bitcast(I32),
                dealt[0][16 * q : 16 * q + 16, :].bitcast(I32),
            )

        def load_w2(a):
            nc.sync.dma_start(w2_raw[a][:].bitcast(I32), w2_words[a].bitcast(I32))

        def load_w3():
            nc.sync.dma_start(w3c[:].bitcast(I32), w3_words.rearrange("a p c i -> p a (c i)").bitcast(I32))
            load_scales(w3s, w3_scales)
            with nc.allow_non_contiguous_dma(reason="one bias value to a partition"):
                nc.sync.dma_start(bias[:], b3.rearrange("(c p) -> p c", p=P))

        def deal_w2_words(a, cb0=0, cb1=2):
            nc.scalar.copy(
                w2c[a][:].bitcast(U16).rearrange("p (b t m) -> p b t m", b=2, t=PACK)[:, cb0:cb1],
                w2_raw[a][:].bitcast(U16).rearrange("p (b m t) -> p b t m", b=2, t=PACK)[:, cb0:cb1],
            )

        def deal_w2_scales():
            dealt[0] = keep.tile([P, KP], U8, name="s2_dealt", tag="wcol", align_bytes=64)
            nc.gpsimd.tensor_copy(
                dealt[0][:].rearrange("p (t m) -> p t m", t=PACK),
                s2_raw[:].rearrange("p (m t) -> p t m", t=PACK),
            )

        def cast(eng, dst, src):
            if eng is nc.scalar:
                nc.scalar.copy(dst, src)
            else:
                nc.vector.tensor_copy(dst, src)

        picked = {
            (1, 0, 1): late[:, 0 : 2 * HALF].rearrange("p (t c) -> p t c", t=2),
            (1, 1, 1): late[:, HALF + UNIT : 3 * HALF + UNIT].rearrange("p (t c) -> p t c", t=2),
        }
        both = {}
        for a, u in ((0, 0), (0, 1), (1, 0)):
            both[a, u] = wide.tile([P, 2 * S], F32, name="both", tag="wide")[:].rearrange("p (t c) -> p t c", t=2)
            for h in range(2):
                picked[a, h, u] = both[a, u][:, :, h * HALF : (h + 1) * HALF]
        for a in range(2):
            for h in range(2):
                xb[a, h] = keep.tile([P, HALF * PACK], BF16, name="xb%d%d" % (a, h), align_bytes=64)[:]

        def gather(a, i, j0, w):
            u, e = divmod(i, 2)
            h, lo = divmod(j0, HALF)
            dst = both[a, u][:, e, :] if w == S else picked[a, h, u][:, e, lo : lo + w]
            nc.vector.tensor_tensor(
                dst,
                planes[a, i][:].indirect(offsets[:, j0 // 16 : (j0 + w) // 16]),
                wg[:, j0 : j0 + w],
                ALU.mult,
            )

        def weave_x(eng, a, h, u, lo=0, w=HALF):
            dst = xb[a, h][:, PACK * lo : PACK * (lo + w)].rearrange("p (c i t) -> p c t i", i=RUN, t=PACK)
            src = picked[a, h, u][:, :, lo : lo + w].rearrange("p t (c i) -> p c t i", i=RUN)
            cast(eng, dst[:, :, 2 * u : 2 * u + 2, :], src)

        def quant_x(a, h):
            tag = {(0, 0): "w2_raw0", (0, 1): "w2_raw1"}.get((a, h), "xc%d%d" % (a, h))
            codes = keep.tile([P, HALF], U32, name="xc", tag=tag, align_bytes=64)
            scales = keep.tile([P, HALF], U8, name="xs%d%d" % (a, h), align_bytes=64)
            xq[a, h] = (codes, scales)
            nc.vector.quantize_mx(codes[:].bitcast(FP8X4), scales[:], xb[a, h])

        def weave_w1(eng, cb, a, tp):
            dst = wb[cb, tp][:, a, :, :, :].rearrange("p t m j -> p m j t")
            src = w1_raw[cb, a][:].rearrange("p j (m t) -> p m j t", t=PACK)[:, :, :, 2 * tp : 2 * tp + 2]
            cast(eng, dst, src)

        def quant_w1(cb, tp):
            codes, scales = w1q[cb, tp]
            nc.vector.quantize_mx(
                codes[:].rearrange("p a c -> p (a c)").bitcast(FP8X4),
                scales[:].rearrange("p a c -> p (a c)"),
                wb[cb, tp][:].rearrange("p a t m j -> p (a t m j)"),
            )

        bbank = {}
        rb = {}

        def b_pass(cb, h, t, a):
            if a == 0:
                n = cb * PACK + t
                bbank[cb, h, t] = bank_tile(RING + (n + 2) % RING if (cb, h) == (1, 1) else n, [P, HALF])
            c0 = cb * KP + t * P
            codes, scales = xq[a, h]
            nc.tensor.matmul_mx(
                bbank[cb, h, t][:],
                lhsT=w2c[a][:, 2 * c0 : 2 * (c0 + P)].bitcast(FP4X4),
                lhsT_scale=w2s[:, cb, a, t * P : (t + 1) * P],
                rhs=codes[:].bitcast(FP8X4),
                rhs_scale=scales[:],
                start=(a == 0),
                stop=(a == 1),
            )

        def relu_b(eng, cb, h, t):
            if t == 0:
                rb[cb, h] = wide.tile([P, PACK, HALF], F32, name="rb", tag="wide")
            if eng is nc.scalar:
                nc.scalar.activation(rb[cb, h][:, t, :], bbank[cb, h, t][:], ACT.Relu)
            else:
                nc.vector.tensor_scalar(rb[cb, h][:, t, :], bbank[cb, h, t][:], 0.0, None, ALU.max)

        def b_tile(eng, cb, h, t):
            b_pass(cb, h, t, 0)
            b_pass(cb, h, t, 1)
            relu_b(eng, cb, h, t)

        diff = {}

        def diff_tiles(tag, w, steps):
            room = keep.tile([P, len(steps), PACK, w], F32, name="diff", tag=tag, align_bytes=64)
            for n, step in enumerate(steps):
                diff[step] = room[:, n, :, :]

        abanks = []
        last = S - P

        def a_sub(cb, j0, w):
            per = HALF // w
            h, jl = divmod(j0, HALF)
            for u in range(PACK // per):
                n = len(abanks)
                bank = bank_tile(A_BANKS[n], [P, per, w])
                abanks.append(bank)
                for v in range(per):
                    tp, tt = divmod(u * per + v, 2)
                    codes, scales = w1q[cb, tp]
                    for a in range(2):
                        xcodes, xscales = xq[a, h]
                        nc.tensor.matmul_mx(
                            bank[:, v, :],
                            lhsT=codes[:, a, tt * P : (tt + 1) * P].bitcast(FP8X4),
                            lhsT_scale=scales[:, a, tt * P : (tt + 1) * P],
                            rhs=xcodes[:, jl : jl + w].bitcast(FP8X4),
                            rhs_scale=xscales[:, jl : jl + w],
                            start=(a == 0),
                            stop=(a == 1),
                        )
                ts = slice(u * per, (u + 1) * per)
                nc.vector.tensor_tensor(diff[cb, j0][:, ts, :], bank[:], rb[cb, h][:, ts, jl : jl + w], ALU.subtract)

        def abs_h(cb, j0, w):
            g, lo = divmod(j0, UNIT)
            nc.scalar.activation(
                hb[g][:, cb, PACK * lo : PACK * (lo + w)].rearrange("p (c i t) -> p c t i", i=RUN, t=PACK),
                diff[cb, j0].rearrange("p t (c i) -> p c t i", i=RUN),
                ACT.Abs,
            )

        def quant_h(g, c0=0, c1=2 * UNIT):
            codes, scales = hq[g]
            nc.vector.quantize_mx(
                codes[:].rearrange("p b c -> p (b c)")[:, c0:c1].bitcast(FP8X4),
                scales[:].rearrange("p b c -> p (b c)")[:, c0:c1],
                hb[g][:].rearrange("p b c -> p (b c)")[:, PACK * c0 : PACK * c1],
            )

        ybank = {}
        res = [keep.tile([P, S], F32, name="res%d" % c) for c in range(N // P)]

        def y_pass(j0, w, c, cb):
            if cb == 0:
                n = len(ybank)
                ybank[j0, c] = bank_tile(LATE_BANKS[n - 6] if n >= 6 else RING + n % RING, [P, w])
            g, lo = divmod(j0, UNIT)
            codes, scales = hq[g]
            nc.tensor.matmul_mx(
                ybank[j0, c][:],
                lhsT=w3c[:, cb, c * P : (c + 1) * P].bitcast(FP8X4),
                lhsT_scale=w3s[:, cb, c * P : (c + 1) * P],
                rhs=codes[:, cb, lo : lo + w].bitcast(FP8X4),
                rhs_scale=scales[:, cb, lo : lo + w],
                start=(cb == 0),
                stop=(cb == 1),
            )

        def y_out(eng, j0, w, c):
            dst = res[c][:, j0 : j0 + w]
            if eng is nc.scalar:
                nc.scalar.activation(dst, ybank[j0, c][:], ACT.Identity, bias=bias[:, c : c + 1])
            else:
                nc.vector.tensor_scalar(dst, ybank[j0, c][:], bias[:, c : c + 1], None, ALU.add)

        def store(j0, w, c):
            nc.sync.dma_start(out[c * P : (c + 1) * P, j0 : j0 + w], res[c][:, j0 : j0 + w])

        def y_tile(eng, j0, w, c):
            y_pass(j0, w, c, 0)
            y_pass(j0, w, c, 1)
            y_out(eng, j0, w, c)

        V, A = nc.vector, nc.scalar

        def h_step(cb, j0, w):
            a_sub(cb, j0, w)
            abs_h(cb, j0, w)

        def y_step(engines, j0, w):
            for c in range(N // P):
                y_tile(engines[c], j0, w, c)
                store(j0, w, c)

        load_wg()
        load_s2()
        load_x(0, 0)
        nc.sync.dma_start(offsets[:], offs)
        for i in range(1, PACK):
            load_x(0, i)
        turn_wg()
        for h in range(2):
            repeat_wg(h)
        deal_w2_scales()
        for q in (0, 2):
            place_s2(nc.scalar, q)
        for h in range(2):
            spread_wg(h)
        for i in range(2):
            load_x(1, i)
        load_w2(0)
        for i in range(2, PACK):
            load_x(1, i)
        for q in (1, 3):
            place_s2(nc.sync, q)
        load_w2(1)

        for i in range(2):
            gather(0, i, 0, S)
        for h in range(2):
            weave_x(A, 0, h, 0)
        gather(0, 2, 0, S)
        for h in range(2):
            gather(0, 3, h * HALF, HALF)
            weave_x(A, 0, h, 1)
        for cb in range(2):
            for a in range(2):
                load_w1(cb, a)
        load_w3()
        deal_w2_words(0)
        gather(1, 0, 0, S)
        for h in range(2):
            gather(1, 1, h * HALF, HALF)
        quant_x(0, 0)
        for h in range(2):
            weave_x(A, 1, h, 0)
        for cb in range(2):
            for t in range(PACK):
                b_pass(cb, 0, t, 0)
        gather(1, 2, 0, HALF)
        gather(1, 2, HALF + UNIT, UNIT)
        for lo, w in LAST_PIECES:
            gather(1, 3, lo, w)
            weave_x(A, 1, 0, 1, lo, w)
        for cb in range(2):
            deal_w2_words(1, cb, cb + 1)
        gather(1, 3, HALF, HALF)
        quant_x(1, 0)
        for cb in range(2):
            for t in range(PACK):
                b_pass(cb, 0, t, 1)
                relu_b(A, cb, 0, t)
        gather(1, 2, HALF, UNIT)
        quant_x(0, 1)
        weave_w1(A, 1, 0, 1)
        for t in range(PACK):
            b_pass(0, 1, t, 0)
        weave_w1(V, 0, 0, 0)
        weave_x(V, 1, 1, 1)
        weave_w1(V, 0, 0, 1)
        quant_x(1, 1)
        for t in range(PACK):
            b_pass(0, 1, t, 1)
            relu_b(A, 0, 1, t)
        b_tile(A, 1, 1, 0)
        for tp in range(2):
            weave_w1(V, 0, 1, tp)
        for tp in range(2):
            quant_w1(0, tp)
        weave_w1(V, 1, 0, 0)
        diff_tiles("plane01", UNIT, [(0, 0)])
        a_sub(0, 0, UNIT)
        for t in range(1, PACK):
            b_tile(A, 1, 1, t)
        abs_h(0, 0, UNIT)
        for tp in range(2):
            weave_w1(V, 1, 1, tp)
        diff_tiles("plane03", UNIT, [(0, UNIT)])
        diff_tiles("plane10", UNIT, [(1, 0), (1, UNIT)])
        diff_tiles("plane11", UNIT, [(0, HALF), (1, HALF)])
        diff_tiles("plane12", UNIT, [(0, HALF + UNIT)])
        diff_tiles("plane13", P, [(1, last - P), (1, last)])
        for tp in range(2):
            quant_w1(1, tp)
        h_step(0, UNIT, UNIT)
        for j0 in (0, UNIT):
            h_step(1, j0, UNIT)
        h_step(0, HALF, UNIT)
        quant_h(0)
        a_sub(1, HALF, UNIT)
        y_step((A, A, A), 0, UNIT)
        abs_h(1, HALF, UNIT)
        quant_h(1)
        a_sub(0, HALF + UNIT, UNIT)
        a_sub(1, last - P, P)
        for c in range(N // P):
            y_pass(UNIT, UNIT, c, 0)
            y_pass(UNIT, UNIT, c, 1)
        y_out(A, UNIT, UNIT, 0)
        store(UNIT, UNIT, 0)
        abs_h(0, HALF + UNIT, UNIT)
        abs_h(1, last - P, P)
        quant_h(2)
        h_step(1, last, P)
        for c in range(1, N // P):
            y_out(V, UNIT, UNIT, c)
            store(UNIT, UNIT, c)
        quant_h(3, 0, UNIT + P)
        for c in range(N // P):
            y_pass(HALF, UNIT, c, 0)
            y_pass(HALF, UNIT, c, 1)
        y_out(V, HALF, UNIT, 0)
        store(HALF, UNIT, 0)
        quant_h(3, UNIT + P, 2 * UNIT)
        for c in range(1, N // P):
            y_out(A, HALF, UNIT, c)
            store(HALF, UNIT, c)
        for c in range(N // P):
            y_tile((A, V, A)[c], last - P, P, c)
        for c in range(N // P):
            y_pass(last, P, c, 0)
        for c in range(N // P):
            y_pass(last, P, c, 1)
            y_out((V, A, V)[c], last, P, c)
            store(last - P, 2 * P, c)
